import numpy as np
import ml_dtypes


def mxq(x, axis, fmt="e4m3"):
    dtype, down = {"e4m3": (ml_dtypes.float8_e4m3fn, 7), "e5m2": (ml_dtypes.float8_e5m2, 14)}[fmt]
    v = np.moveaxis(np.asarray(x, np.float32).astype(ml_dtypes.bfloat16).astype(np.float64), axis, -1)
    blocks = v.reshape(v.shape[:-1] + (-1, 32))
    amax = np.abs(blocks).max(-1, keepdims=True)
    byte = np.maximum(np.where(amax > 0, np.frexp(amax)[1] - 1 + 127, 0) - down, 1)
    scale = np.exp2(byte - 127.0)
    codes = (blocks / scale).astype(np.float32).astype(dtype).astype(np.float64)
    return np.moveaxis((codes * scale).reshape(v.shape), -1, axis)


WIDE = False


def mx_kscale(k):
    if not WIDE:
        return np.ones(k)
    levels = np.array([10, -10, 5, -5, 0])
    if k % 512:
        return np.exp2(np.random.permutation(np.resize(levels, k // 32))).repeat(32)
    a = np.empty((k // 512, 16))
    for p in range(k // 512):
        a[p, :8] = np.random.permutation(np.resize(levels, 8))
        for g in range(8):
            far = levels[np.abs(levels - a[p, g]) >= 10]
            a[p, g + 8] = far[np.random.randint(len(far))]
    return np.exp2(a.ravel()).repeat(32)


def f64(x):
    return np.asarray(x).astype(np.float64)


def striped(idx):
    return np.tile(idx.reshape(-1, 16).T, (8, 1)).astype(np.uint16)


def unstriped(offs):
    return offs[:16].T.reshape(-1).astype(np.int64)


def striped8(idx):
    return np.concatenate([x.reshape(-1, 16).T for x in idx]).astype(np.uint16)


def runs(offs, k):
    lists = np.stack([offs[16 * r : 16 * r + 16].T.reshape(-1) for r in range(8)]).astype(np.int64)
    return lists[np.arange(k) % 512 // 64]


def pack_weight(w):
    k, n = w.shape
    w = f64(np.asarray(w, np.float32).astype(ml_dtypes.bfloat16)).reshape(k // 32, 32, n)
    amax = np.abs(w).max(1)
    byte = np.clip(np.where(amax > 0, np.frexp(amax)[1] - 1 + 127 - 7, 1), 1, 254)
    scaled = (w * np.exp2(127.0 - byte)[:, None, :]).reshape(k, n).astype(np.float32)
    words = np.ascontiguousarray(scaled.reshape(k // 512, 128, 4, n).transpose(0, 1, 3, 2)).astype(ml_dtypes.float8_e4m3fn).view(np.uint8)
    return words, np.ascontiguousarray(byte.astype(np.uint8).reshape(k // 512, 16, n))


def unpack_weight(words, scales):
    g, p, n, _ = words.shape
    vals = np.ascontiguousarray(words).view(ml_dtypes.float8_e4m3fn).astype(np.float64) * np.repeat(np.exp2(scales.astype(np.float64) - 127.0), 8, axis=1)[..., None]
    return vals.transpose(0, 1, 3, 2).reshape(g * 512, n)


K, T, S, V, N, H = 512, 2048, 1024, 512, 512, 512


def setup_inputs():
    n = np.random.standard_normal
    s = mx_kscale(K)[:, None]
    u = mx_kscale(H)
    packed_xT = pack_weight(n((K, T)) * s)
    return {
        "x_words": packed_xT[0],
        "x_scales": packed_xT[1],
        "w1": (n((K, H)) / np.sqrt(K) / s).astype(np.float32),
        "gl": (np.random.uniform(0.5, 1.5, (H, 1)) * u[:, None]).astype(np.float32),
        "gh": (np.random.uniform(0.5, 1.5, (H, 1)) * u[:, None]).astype(np.float32),
        "w2": (n((H, N)) / np.sqrt(2 * H) / u[:, None]).astype(np.float32),
        "w3": (n((H, N)) / np.sqrt(2 * H) / u[:, None]).astype(np.float32),
        "offs": striped(np.random.permutation(T)[:S]),
        "left": striped8(np.stack([np.random.permutation(S)[:V] for _ in range(8)])),
        "right": striped8(np.stack([np.random.permutation(S)[:V] for _ in range(8)])),
    }


def reference(x_words, x_scales, w1, gl, gh, w2, w3, offs, left, right):
    xq = unpack_weight(x_words, x_scales)[:, unstriped(offs)]
    y = mxq(f64(w1), 0, "e4m3").T @ xq
    lf = y[np.arange(H)[:, None], runs(left, H)]
    rt = y[np.arange(H)[:, None], runs(right, H)]
    z = f64(gl) * (lf + rt)
    d = 0.75 * (lf - rt)
    z2 = f64(gh) * (d - np.clip(d, -0.5, 0.5))
    return mxq(f64(w2), 0, "e4m3").T @ mxq(z, 0, "e4m3") + mxq(f64(w3), 0, "e4m3").T @ mxq(z2, 0, "e4m3")

@@ -1,0 +1,201 @@
+from contextlib import ExitStack
+
+import concourse.mybir as mybir
+
+K, T, S, V, N, H = 512, 2048, 1024, 512, 512, 512
+FLOPS = 2 * K * H * S + 2 * 2 * H * N * V
+
+F32 = mybir.dt.float32
+BF16 = mybir.dt.bfloat16
+I32 = mybir.dt.int32
+U32 = mybir.dt.uint32
+U16 = mybir.dt.uint16
+U8 = mybir.dt.uint8
+FP8X4 = mybir.dt.float8_e4m3fn_x4
+ALU = mybir.AluOpType
+ACT = mybir.ActivationFunctionType
+
+P = 128
+PACK = 4
+BANK = 512
+CHUNKS = ((0, 256), (256, 128), (384, 128))
+
+
+def tile_picked_haarthr_none_p_kernel(
+    tc, x_words, x_scales, w1, gl, gh, w2, w3, offs, left, right, out
+):
+    nc = tc.nc
+    with ExitStack() as ctx:
+        keep = ctx.enter_context(tc.tile_pool(name="keep", bufs=1))
+        psum = ctx.enter_context(tc.psum_pool(name="psum", bufs=8))
+
+        offs_sb = keep.tile([P, S // 16], U16, name="offs_sb")
+        left_sb = keep.tile([P, V // 16], U16, name="left_sb")
+        right_sb = keep.tile([P, V // 16], U16, name="right_sb")
+        nc.sync.dma_start(offs_sb[:], offs)
+
+        x_scale_sb = keep.tile([P, T], U8, name="x_scale_sb", align_bytes=64)
+        nc.vector.memset(x_scale_sb[:].bitcast(I32), 0)
+        for q in range(4):
+            nc.scalar.dma_start(
+                x_scale_sb[32 * q : 32 * q + 4, :].bitcast(I32), x_scales[0, 4 * q : 4 * q + 4, :].bitcast(I32)
+            )
+        x_word_sb = keep.tile([P, T], U32, name="x_word_sb", align_bytes=64)
+        nc.sync.dma_start(x_word_sb[:].bitcast(I32), x_words[0].rearrange("p c r -> p (c r)").bitcast(I32))
+
+        gl_sb = keep.tile([P, PACK], F32, name="gl_sb")
+        gh_sb = keep.tile([P, PACK], F32, name="gh_sb")
+
+        w1_rows = w1.rearrange("(p j) c -> p j c", j=PACK)
+        w1_raw = []
+        for half in range(2):
+            raw = keep.tile([P, PACK, H // 2], F32, name=f"w1_raw{half}")
+            nc.sync.dma_start(raw[:], w1_rows[:, :, half * (H // 2) : (half + 1) * (H // 2)])
+            w1_raw.append(raw)
+        nc.sync.dma_start(gl_sb[:], gl.rearrange("(p t) o -> p (t o)", t=PACK))
+        nc.sync.dma_start(gh_sb[:], gh.rearrange("(p t) o -> p (t o)", t=PACK))
+        nc.sync.dma_start(left_sb[:], left)
+        nc.sync.dma_start(right_sb[:], right)
+        w2_raw = keep.tile([P, PACK, N], F32, name="w2_raw")
+        w3_raw = keep.tile([P, PACK, N], F32, name="w3_raw")
+        nc.sync.dma_start(w2_raw[:], w2.rearrange("(p j) c -> p j c", j=PACK))
+        nc.sync.dma_start(w3_raw[:], w3.rearrange("(p j) c -> p j c", j=PACK))
+
+        xq_scale = keep.tile([P, S], U8, name="xq_scale", align_bytes=64)
+        xq_word = keep.tile([P, S], U32, name="xq_word", align_bytes=64)
+        nc.vector.tensor_copy(xq_scale[:], x_scale_sb[:].indirect(offs_sb[:]))
+        nc.vector.tensor_copy(xq_word[:], x_word_sb[:].indirect(offs_sb[:]))
+
+        w1_bf = keep.tile([P, PACK, P, PACK], BF16, name="w1_bf", align_bytes=64)
+        for half in range(2):
+            nc.scalar.copy(
+                w1_bf[:, :, half * (P // 2) : (half + 1) * (P // 2), :].rearrange("p t m j -> p m j t"),
+                w1_raw[half][:].rearrange("p j (m t) -> p m j t", t=PACK),
+            )
+        gl_twice = keep.tile([P, PACK], F32, name="gl_twice")
+        slope = keep.tile([P, PACK], F32, name="slope")
+        slope_neg = keep.tile([P, PACK], F32, name="slope_neg")
+        knee = keep.tile([P, PACK], F32, name="knee")
+        knee_neg = keep.tile([P, PACK], F32, name="knee_neg")
+        nc.scalar.activation(gl_twice[:], gl_sb[:], ACT.Copy, scale=2.0)
+        nc.scalar.activation(slope[:], gh_sb[:], ACT.Copy, scale=0.75)
+        nc.scalar.activation(slope_neg[:], gh_sb[:], ACT.Copy, scale=-0.75)
+        nc.scalar.activation(knee[:], gh_sb[:], ACT.Abs, scale=0.5)
+        nc.scalar.activation(knee_neg[:], knee[:], ACT.Copy, scale=-1.0)
+
+        w1_word = keep.tile([P, H], U32, name="w1_word", align_bytes=64)
+        w1_scale = keep.tile([P, H], U8, name="w1_scale", align_bytes=64)
+        for t in range(PACK):
+            cols = slice(t * P, (t + 1) * P)
+            nc.vector.quantize_mx(
+                out=w1_word[:, cols].bitcast(FP8X4),
+                scales=w1_scale[:, cols],
+                in_=w1_bf[:, t].rearrange("p m j -> p (m j)"),
+            )
+
+        y = [keep.tile([P, S], F32, name=f"y{t}") for t in range(PACK)]
+        for t in range(PACK):
+            cols = slice(t * P, (t + 1) * P)
+            for half in range(S // BANK):
+                tok = slice(half * BANK, (half + 1) * BANK)
+                acc = psum.tile([P, BANK], F32, name="acc")
+                nc.tensor.matmul_mx(
+                    out=acc[:],
+                    lhsT=w1_word[:, cols].bitcast(FP8X4),
+                    lhsT_scale=w1_scale[:, cols],
+                    rhs=xq_word[:, tok].bitcast(FP8X4),
+                    rhs_scale=xq_scale[:, tok],
+                    start=True,
+                    stop=True,
+                )
+                if (t, half) == (0, 1):
+                    nc.vector.tensor_copy(y[t][:, tok], acc[:])
+                else:
+                    nc.scalar.copy(y[t][:, tok], acc[:])
+
+        lf = [keep.tile([P, V], F32, name=f"lf{t}") for t in range(PACK)]
+        dn = [keep.tile([P, V], F32, name=f"dn{t}") for t in range(PACK)]
+        parts = {}
+        for c, (v0, n) in enumerate(CHUNKS):
+            for name in ("lo_a", "lo_b", "hi_a", "hi_b"):
+                parts[name, c] = keep.tile([P, PACK, n], F32, name=f"{name}{c}")
+
+        def scale_parts(t, c):
+            v0, n = CHUNKS[c]
+            cols = slice(v0, v0 + n)
+            one = slice(t, t + 1)
+            nc.scalar.activation(parts["lo_a", c][:, t, :], lf[t][:, cols], ACT.Copy, scale=gl_twice[:, one])
+            nc.scalar.activation(parts["lo_b", c][:, t, :], dn[t][:, cols], ACT.Copy, scale=gl_sb[:, one])
+            nc.scalar.activation(
+                parts["hi_a", c][:, t, :], dn[t][:, cols], ACT.Relu, scale=slope_neg[:, one], bias=knee_neg[:, one]
+            )
+            nc.scalar.activation(
+                parts["hi_b", c][:, t, :], dn[t][:, cols], ACT.Relu, scale=slope[:, one], bias=knee_neg[:, one]
+            )
+
+        def interleave(raw, name, copy):
+            grouped = keep.tile([P, N, PACK], BF16, name=name, align_bytes=64)
+            copy(
+                grouped[:].rearrange("p (c i) j -> p c j i", i=4), raw[:].rearrange("p j (c i) -> p c j i", i=4)
+            )
+            return grouped
+
+        def quantize(grouped, width, name):
+            word = keep.tile([P, width], U32, name=f"{name}_word", align_bytes=64)
+            scale = keep.tile([P, width], U8, name=f"{name}_scale", align_bytes=64)
+            nc.vector.quantize_mx(
+                out=word[:].bitcast(FP8X4), scales=scale[:], in_=grouped[:].rearrange("p w j -> p (w j)")
+            )
+            return word, scale
+
+        for t in range(PACK):
+            nc.vector.tensor_copy(lf[t][:], y[t][:].indirect(left_sb[:]))
+            nc.vector.tensor_tensor(dn[t][:], y[t][:].indirect(right_sb[:]), lf[t][:], ALU.subtract)
+            scale_parts(t, 0)
+            if t == 1:
+                w2_bf = interleave(w2_raw, "w2_bf", nc.scalar.copy)
+            elif t < PACK - 1:
+                for c in range(1, len(CHUNKS)):
+                    scale_parts(t, c)
+        w3_bf = interleave(w3_raw, "w3_bf", nc.vector.tensor_copy)
+        w2_q = quantize(w2_bf, N, "w2")
+        w3_q = quantize(w3_bf, N, "w3")
+        for c in range(1, len(CHUNKS)):
+            for t in (1, PACK - 1):
+                scale_parts(t, c)
+
+        def combine(first, second, op, n, name):
+            grouped = keep.tile([P, n, PACK], BF16, name=name, align_bytes=64)
+            nc.vector.tensor_tensor(
+                grouped[:].rearrange("p (c i) t -> p c t i", i=4),
+                first[:].rearrange("p t (c i) -> p c t i", i=4),
+                second[:].rearrange("p t (c i) -> p c t i", i=4),
+                op,
+            )
+            return grouped
+
+        for c, (v0, n) in enumerate(CHUNKS):
+            z_bf = combine(parts["lo_a", c], parts["lo_b", c], ALU.add, n, f"z_bf{c}")
+            z2_bf = combine(parts["hi_a", c], parts["hi_b", c], ALU.subtract, n, f"z2_bf{c}")
+            z_q = quantize(z_bf, n, f"z{c}")
+            z2_q = quantize(z2_bf, n, f"z2{c}")
+            accs = [psum.tile([P, n], F32, name="acc") for m in range(N // P)]
+            for first, (w_q, act_q) in ((True, (w2_q, z_q)), (False, (w3_q, z2_q))):
+                for m in range(N // P):
+                    cols = slice(m * P, (m + 1) * P)
+                    nc.tensor.matmul_mx(
+                        out=accs[m][:],
+                        lhsT=w_q[0][:, cols].bitcast(FP8X4),
+                        lhsT_scale=w_q[1][:, cols],
+                        rhs=act_q[0][:].bitcast(FP8X4),
+                        rhs_scale=act_q[1][:],
+                        start=first,
+                        stop=not first,
+                    )
+            for m in range(N // P):
+                res = keep.tile([P, n], F32, name=f"res{c}_{m}")
+                if c == len(CHUNKS) - 1 and m % 2 == 1:
+                    nc.vector.tensor_copy(res[:], accs[m][:])
+                else:
+                    nc.scalar.copy(res[:], accs[m][:])
+                nc.sync.dma_start(out[m * P : (m + 1) * P, v0 : v0 + n], res[:])

@@ -35,30 +35,32 @@ def tile_picked_haarthr_none_p_kernel(
         nc.sync.dma_start(offs_sb[:], offs)
 
         x_scale_sb = keep.tile([P, T], U8, name="x_scale_sb", align_bytes=64)
-        nc.vector.memset(x_scale_sb[:].bitcast(I32), 0)
-        for q in range(4):
-            nc.scalar.dma_start(
-                x_scale_sb[32 * q : 32 * q + 4, :].bitcast(I32), x_scales[0, 4 * q : 4 * q + 4, :].bitcast(I32)
-            )
         x_word_sb = keep.tile([P, T], U32, name="x_word_sb", align_bytes=64)
-        nc.sync.dma_start(x_word_sb[:].bitcast(I32), x_words[0].rearrange("p c r -> p (c r)").bitcast(I32))
-
         gl_sb = keep.tile([P, PACK], F32, name="gl_sb")
         gh_sb = keep.tile([P, PACK], F32, name="gh_sb")
-
+        w1_raw = [keep.tile([P, PACK, H // 2], F32, name=f"w1_raw{half}") for half in range(2)]
         w1_rows = w1.rearrange("(p j) c -> p j c", j=PACK)
-        w1_raw = []
-        for half in range(2):
-            raw = keep.tile([P, PACK, H // 2], F32, name=f"w1_raw{half}")
-            nc.sync.dma_start(raw[:], w1_rows[:, :, half * (H // 2) : (half + 1) * (H // 2)])
-            w1_raw.append(raw)
-        nc.sync.dma_start(gl_sb[:], gl.rearrange("(p t) o -> p (t o)", t=PACK))
+
+        w2_raw = [keep.tile([P, PACK, N // 2], F32, name=f"w2_raw{half}") for half in range(2)]
+        w2_rows = w2.rearrange("(p j) c -> p j c", j=PACK)
+        w3_raw = keep.tile([P, PACK, N], F32, name="w3_raw")
+        x_rows = x_words[0].rearrange("p c r -> p (c r)").bitcast(I32)
+
+        nc.vector.memset(x_scale_sb[:].bitcast(I32), 0)
+        nc.sync.dma_start(x_word_sb[:, : T // 2].bitcast(I32), x_rows[:, : T // 2])
         nc.sync.dma_start(gh_sb[:], gh.rearrange("(p t) o -> p (t o)", t=PACK))
+        for q in range(4):
+            nc.sync.dma_start(
+                x_scale_sb[32 * q : 32 * q + 4, :].bitcast(I32), x_scales[0, 4 * q : 4 * q + 4, :].bitcast(I32)
+            )
+        nc.sync.dma_start(x_word_sb[:, T // 2 :].bitcast(I32), x_rows[:, T // 2 :])
+        for half in range(2):
+            nc.sync.dma_start(w1_raw[half][:], w1_rows[:, :, half * (H // 2) : (half + 1) * (H // 2)])
+        nc.sync.dma_start(gl_sb[:], gl.rearrange("(p t) o -> p (t o)", t=PACK))
+        for half in range(2):
+            nc.sync.dma_start(w2_raw[half][:], w2_rows[:, :, half * (N // 2) : (half + 1) * (N // 2)])
         nc.sync.dma_start(left_sb[:], left)
         nc.sync.dma_start(right_sb[:], right)
-        w2_raw = keep.tile([P, PACK, N], F32, name="w2_raw")
-        w3_raw = keep.tile([P, PACK, N], F32, name="w3_raw")
-        nc.sync.dma_start(w2_raw[:], w2.rearrange("(p j) c -> p j c", j=PACK))
         nc.sync.dma_start(w3_raw[:], w3.rearrange("(p j) c -> p j c", j=PACK))
 
         xq_scale = keep.tile([P, S], U8, name="xq_scale", align_bytes=64)
@@ -96,22 +98,19 @@ def tile_picked_haarthr_none_p_kernel(
         y = [keep.tile([P, S], F32, name=f"y{t}") for t in range(PACK)]
         for t in range(PACK):
             cols = slice(t * P, (t + 1) * P)
-            for half in range(S // BANK):
-                tok = slice(half * BANK, (half + 1) * BANK)
-                acc = psum.tile([P, BANK], F32, name="acc")
+            width = BANK // 2 if t == 0 else BANK
+            for s0, s1 in ((s, s + width) for s in range(0, S, width)):
+                acc = psum.tile([P, s1 - s0], F32, name="acc")
                 nc.tensor.matmul_mx(
                     out=acc[:],
                     lhsT=w1_word[:, cols].bitcast(FP8X4),
                     lhsT_scale=w1_scale[:, cols],
-                    rhs=xq_word[:, tok].bitcast(FP8X4),
-                    rhs_scale=xq_scale[:, tok],
+                    rhs=xq_word[:, s0:s1].bitcast(FP8X4),
+                    rhs_scale=xq_scale[:, s0:s1],
                     start=True,
                     stop=True,
                 )
-                if (t, half) == (0, 1):
-                    nc.vector.tensor_copy(y[t][:, tok], acc[:])
-                else:
-                    nc.scalar.copy(y[t][:, tok], acc[:])
+                nc.scalar.copy(y[t][:, s0:s1], acc[:])
 
         lf = [keep.tile([P, V], F32, name=f"lf{t}") for t in range(PACK)]
         dn = [keep.tile([P, V], F32, name=f"dn{t}") for t in range(PACK)]
@@ -148,20 +147,33 @@ def tile_picked_haarthr_none_p_kernel(
             )
             return word, scale
 
+        w2_bf = keep.tile([P, N, PACK], BF16, name="w2_bf", align_bytes=64)
+        for half in range(2):
+            nc.vector.tensor_copy(
+                w2_bf[:, half * (N // 2) : (half + 1) * (N // 2), :].rearrange("p (c i) j -> p c j i", i=4),
+                w2_raw[half][:].rearrange("p j (c i) -> p c j i", i=4),
+            )
         for t in range(PACK):
-            nc.vector.tensor_copy(lf[t][:], y[t][:].indirect(left_sb[:]))
-            nc.vector.tensor_tensor(dn[t][:], y[t][:].indirect(right_sb[:]), lf[t][:], ALU.subtract)
+            for h in range(2):
+                nc.vector.tensor_copy(
+                    lf[t][:, h * 256 : (h + 1) * 256], y[t][:].indirect(left_sb[:, h * 16 : (h + 1) * 16])
+                )
+            for h in range(2):
+                nc.vector.tensor_tensor(
+                    dn[t][:, h * 256 : (h + 1) * 256],
+                    y[t][:].indirect(right_sb[:, h * 16 : (h + 1) * 16]),
+                    lf[t][:, h * 256 : (h + 1) * 256],
+                    ALU.subtract,
+                )
             scale_parts(t, 0)
-            if t == 1:
-                w2_bf = interleave(w2_raw, "w2_bf", nc.scalar.copy)
-            elif t < PACK - 1:
+            if t == 0:
                 for c in range(1, len(CHUNKS)):
                     scale_parts(t, c)
-        w3_bf = interleave(w3_raw, "w3_bf", nc.vector.tensor_copy)
+            if t == 1:
+                w3_bf = interleave(w3_raw, "w3_bf", nc.scalar.copy)
         w2_q = quantize(w2_bf, N, "w2")
-        w3_q = quantize(w3_bf, N, "w3")
         for c in range(1, len(CHUNKS)):
-            for t in (1, PACK - 1):
+            for t in range(1, PACK):
                 scale_parts(t, c)
 
         def combine(first, second, op, n, name):
@@ -174,28 +186,39 @@ def tile_picked_haarthr_none_p_kernel(
             )
             return grouped
 
-        for c, (v0, n) in enumerate(CHUNKS):
-            z_bf = combine(parts["lo_a", c], parts["lo_b", c], ALU.add, n, f"z_bf{c}")
-            z2_bf = combine(parts["hi_a", c], parts["hi_b", c], ALU.subtract, n, f"z2_bf{c}")
-            z_q = quantize(z_bf, n, f"z{c}")
-            z2_q = quantize(z2_bf, n, f"z2{c}")
-            accs = [psum.tile([P, n], F32, name="acc") for m in range(N // P)]
-            for first, (w_q, act_q) in ((True, (w2_q, z_q)), (False, (w3_q, z2_q))):
-                for m in range(N // P):
-                    cols = slice(m * P, (m + 1) * P)
-                    nc.tensor.matmul_mx(
-                        out=accs[m][:],
-                        lhsT=w_q[0][:, cols].bitcast(FP8X4),
-                        lhsT_scale=w_q[1][:, cols],
-                        rhs=act_q[0][:].bitcast(FP8X4),
-                        rhs_scale=act_q[1][:],
-                        start=first,
-                        stop=not first,
-                    )
+        def product(accs, w_q, act_q, first):
+            for m in range(N // P):
+                cols = slice(m * P, (m + 1) * P)
+                nc.tensor.matmul_mx(
+                    out=accs[m][:],
+                    lhsT=w_q[0][:, cols].bitcast(FP8X4),
+                    lhsT_scale=w_q[1][:, cols],
+                    rhs=act_q[0][:].bitcast(FP8X4),
+                    rhs_scale=act_q[1][:],
+                    start=first,
+                    stop=not first,
+                )
+
+        def finish(c, accs, z2_bf):
+            v0, n = CHUNKS[c]
+            product(accs, w3_q, quantize(z2_bf, n, f"z2{c}"), False)
+            last = c == len(CHUNKS) - 1
             for m in range(N // P):
                 res = keep.tile([P, n], F32, name=f"res{c}_{m}")
-                if c == len(CHUNKS) - 1 and m % 2 == 1:
+                if last and m % 2 == 1:
                     nc.vector.tensor_copy(res[:], accs[m][:])
                 else:
                     nc.scalar.copy(res[:], accs[m][:])
-                nc.sync.dma_start(out[m * P : (m + 1) * P, v0 : v0 + n], res[:])
+                queue = nc.scalar if last and m % 2 == 0 else nc.sync
+                queue.dma_start(out[m * P : (m + 1) * P, v0 : v0 + n], res[:])
+
+        for c, (v0, n) in enumerate(CHUNKS):
+            z_bf = combine(parts["lo_a", c], parts["lo_b", c], ALU.add, n, f"z_bf{c}")
+            if c == 0:
+                w3_q = quantize(w3_bf, N, "w3")
+            else:
+                finish(c - 1, accs, z2_bf)
+            accs = [psum.tile([P, n], F32, name="acc") for m in range(N // P)]
+            product(accs, w2_q, quantize(z_bf, n, f"z{c}"), True)
+            z2_bf = combine(parts["hi_a", c], parts["hi_b", c], ALU.subtract, n, f"z2_bf{c}")
+        finish(len(CHUNKS) - 1, accs, z2_bf)

@@ -18,6 +18,10 @@ ACT = mybir.ActivationFunctionType
 P = 128
 PACK = 4
 BANK = 512
+HALF = V // 2
+HALF_BYTES = PACK * HALF * 4
+X_HEAD = 640
+POOL_TERMS = 2
 CHUNKS = ((0, 256), (256, 128), (384, 128))
 
 
@@ -27,7 +31,8 @@ def tile_picked_haarthr_none_p_kernel(
     nc = tc.nc
     with ExitStack() as ctx:
         keep = ctx.enter_context(tc.tile_pool(name="keep", bufs=1))
-        psum = ctx.enter_context(tc.psum_pool(name="psum", bufs=8))
+        reuse = ctx.enter_context(tc.tile_pool(name="reuse", bufs=1))
+        psum = ctx.enter_context(tc.psum_pool(name="psum", bufs=1))
 
         offs_sb = keep.tile([P, S // 16], U16, name="offs_sb")
         left_sb = keep.tile([P, V // 16], U16, name="left_sb")
@@ -41,27 +46,31 @@ def tile_picked_haarthr_none_p_kernel(
         w1_raw = [keep.tile([P, PACK, H // 2], F32, name=f"w1_raw{half}") for half in range(2)]
         w1_rows = w1.rearrange("(p j) c -> p j c", j=PACK)
 
-        w2_raw = [keep.tile([P, PACK, N // 2], F32, name=f"w2_raw{half}") for half in range(2)]
+        w2_raw = [keep.tile([P, PACK, N // 2], F32, name=f"w2_raw{half}", tag=f"w2_then_y{half}") for half in range(2)]
         w2_rows = w2.rearrange("(p j) c -> p j c", j=PACK)
-        w3_raw = keep.tile([P, PACK, N], F32, name="w3_raw")
+        w3_raw = [
+            keep.tile([P, PACK, N // 2], F32, name=f"w3_raw{half}") for half in range(2)
+        ]
+        w3_rows = w3.rearrange("(p j) c -> p j c", j=PACK)
         x_rows = x_words[0].rearrange("p c r -> p (c r)").bitcast(I32)
 
         nc.vector.memset(x_scale_sb[:].bitcast(I32), 0)
-        nc.sync.dma_start(x_word_sb[:, : T // 2].bitcast(I32), x_rows[:, : T // 2])
+        nc.sync.dma_start(x_word_sb[:, :X_HEAD].bitcast(I32), x_rows[:, :X_HEAD])
         nc.sync.dma_start(gh_sb[:], gh.rearrange("(p t) o -> p (t o)", t=PACK))
         for q in range(4):
             nc.sync.dma_start(
                 x_scale_sb[32 * q : 32 * q + 4, :].bitcast(I32), x_scales[0, 4 * q : 4 * q + 4, :].bitcast(I32)
             )
-        nc.sync.dma_start(x_word_sb[:, T // 2 :].bitcast(I32), x_rows[:, T // 2 :])
+        nc.sync.dma_start(x_word_sb[:, X_HEAD:].bitcast(I32), x_rows[:, X_HEAD:])
         for half in range(2):
             nc.sync.dma_start(w1_raw[half][:], w1_rows[:, :, half * (H // 2) : (half + 1) * (H // 2)])
         nc.sync.dma_start(gl_sb[:], gl.rearrange("(p t) o -> p (t o)", t=PACK))
+        nc.sync.dma_start(left_sb[:], left)
         for half in range(2):
             nc.sync.dma_start(w2_raw[half][:], w2_rows[:, :, half * (N // 2) : (half + 1) * (N // 2)])
-        nc.sync.dma_start(left_sb[:], left)
+        for half in range(2):
+            nc.sync.dma_start(w3_raw[half][:], w3_rows[:, :, half * (N // 2) : (half + 1) * (N // 2)])
         nc.sync.dma_start(right_sb[:], right)
-        nc.sync.dma_start(w3_raw[:], w3.rearrange("(p j) c -> p j c", j=PACK))
 
         xq_scale = keep.tile([P, S], U8, name="xq_scale", align_bytes=64)
         xq_word = keep.tile([P, S], U32, name="xq_word", align_bytes=64)
@@ -75,116 +84,108 @@ def tile_picked_haarthr_none_p_kernel(
                 w1_raw[half][:].rearrange("p j (m t) -> p m j t", t=PACK),
             )
         gl_twice = keep.tile([P, PACK], F32, name="gl_twice")
+        gl_twice_pool = reuse.tile([P, 16], F32, name="gl_twice_pool", offset=HALF_BYTES - 32)
         slope = keep.tile([P, PACK], F32, name="slope")
         slope_neg = keep.tile([P, PACK], F32, name="slope_neg")
         knee = keep.tile([P, PACK], F32, name="knee")
         knee_neg = keep.tile([P, PACK], F32, name="knee_neg")
         nc.scalar.activation(gl_twice[:], gl_sb[:], ACT.Copy, scale=2.0)
+        nc.scalar.activation(gl_twice_pool[:, :PACK], gl_sb[:], ACT.Copy, scale=2.0)
         nc.scalar.activation(slope[:], gh_sb[:], ACT.Copy, scale=0.75)
         nc.scalar.activation(slope_neg[:], gh_sb[:], ACT.Copy, scale=-0.75)
         nc.scalar.activation(knee[:], gh_sb[:], ACT.Abs, scale=0.5)
         nc.scalar.activation(knee_neg[:], knee[:], ACT.Copy, scale=-1.0)
 
-        w1_word = keep.tile([P, H], U32, name="w1_word", align_bytes=64)
+        w1_word = reuse.tile([P, H], U32, name="w1_word", align_bytes=64, offset=3 * HALF_BYTES)
         w1_scale = keep.tile([P, H], U8, name="w1_scale", align_bytes=64)
-        for t in range(PACK):
-            cols = slice(t * P, (t + 1) * P)
+        for t0, t1 in ((0, 1), (1, 2), (2, 4)):
+            cols = slice(t0 * P, t1 * P)
             nc.vector.quantize_mx(
                 out=w1_word[:, cols].bitcast(FP8X4),
                 scales=w1_scale[:, cols],
-                in_=w1_bf[:, t].rearrange("p m j -> p (m j)"),
+                in_=w1_bf[:, t0:t1].rearrange("p t m j -> p (t m j)"),
             )
-
-        y = [keep.tile([P, S], F32, name=f"y{t}") for t in range(PACK)]
-        for t in range(PACK):
-            cols = slice(t * P, (t + 1) * P)
-            width = BANK // 2 if t == 0 else BANK
-            for s0, s1 in ((s, s + width) for s in range(0, S, width)):
-                acc = psum.tile([P, s1 - s0], F32, name="acc")
-                nc.tensor.matmul_mx(
-                    out=acc[:],
-                    lhsT=w1_word[:, cols].bitcast(FP8X4),
-                    lhsT_scale=w1_scale[:, cols],
-                    rhs=xq_word[:, s0:s1].bitcast(FP8X4),
-                    rhs_scale=xq_scale[:, s0:s1],
-                    start=True,
-                    stop=True,
-                )
-                nc.scalar.copy(y[t][:, s0:s1], acc[:])
-
-        lf = [keep.tile([P, V], F32, name=f"lf{t}") for t in range(PACK)]
-        dn = [keep.tile([P, V], F32, name=f"dn{t}") for t in range(PACK)]
-        parts = {}
-        for c, (v0, n) in enumerate(CHUNKS):
-            for name in ("lo_a", "lo_b", "hi_a", "hi_b"):
-                parts[name, c] = keep.tile([P, PACK, n], F32, name=f"{name}{c}")
-
-        def scale_parts(t, c):
-            v0, n = CHUNKS[c]
-            cols = slice(v0, v0 + n)
-            one = slice(t, t + 1)
-            nc.scalar.activation(parts["lo_a", c][:, t, :], lf[t][:, cols], ACT.Copy, scale=gl_twice[:, one])
-            nc.scalar.activation(parts["lo_b", c][:, t, :], dn[t][:, cols], ACT.Copy, scale=gl_sb[:, one])
-            nc.scalar.activation(
-                parts["hi_a", c][:, t, :], dn[t][:, cols], ACT.Relu, scale=slope_neg[:, one], bias=knee_neg[:, one]
-            )
-            nc.scalar.activation(
-                parts["hi_b", c][:, t, :], dn[t][:, cols], ACT.Relu, scale=slope[:, one], bias=knee_neg[:, one]
-            )
-
-        def interleave(raw, name, copy):
-            grouped = keep.tile([P, N, PACK], BF16, name=name, align_bytes=64)
-            copy(
-                grouped[:].rearrange("p (c i) j -> p c j i", i=4), raw[:].rearrange("p j (c i) -> p c j i", i=4)
-            )
-            return grouped
 
         def quantize(grouped, width, name):
             word = keep.tile([P, width], U32, name=f"{name}_word", align_bytes=64)
             scale = keep.tile([P, width], U8, name=f"{name}_scale", align_bytes=64)
-            nc.vector.quantize_mx(
-                out=word[:].bitcast(FP8X4), scales=scale[:], in_=grouped[:].rearrange("p w j -> p (w j)")
-            )
+            nc.vector.quantize_mx(out=word[:].bitcast(FP8X4), scales=scale[:], in_=grouped)
             return word, scale
 
-        w2_bf = keep.tile([P, N, PACK], BF16, name="w2_bf", align_bytes=64)
-        for half in range(2):
-            nc.vector.tensor_copy(
+        w2_bf = keep.tile([P, N, PACK], BF16, name="w2_bf", tag="w_bf", align_bytes=64)
+        for half, copy in enumerate((nc.scalar.copy, nc.vector.tensor_copy)):
+            copy(
                 w2_bf[:, half * (N // 2) : (half + 1) * (N // 2), :].rearrange("p (c i) j -> p c j i", i=4),
                 w2_raw[half][:].rearrange("p j (c i) -> p c j i", i=4),
             )
+        w2_q = quantize(w2_bf[:].rearrange("p w j -> p (w j)"), N, "w2")
+
+        y = [keep.tile([P, S], F32, name=f"y{t}", tag=f"w2_then_y{t}") for t in range(PACK)]
+        steps = [(0, s0, s0 + BANK // 2) for s0 in range(0, S, BANK // 2)]
+        steps = steps + [(t, s0, s0 + BANK) for t in range(1, PACK) for s0 in (0, BANK)]
+        for step, (t, s0, s1) in enumerate(steps):
+            cols = slice(t * P, (t + 1) * P)
+            acc = psum.tile([P, s1 - s0], F32, name=f"y_acc{step}", tag=f"bank{step % 4}")
+            nc.tensor.matmul_mx(
+                out=acc[:],
+                lhsT=w1_word[:, cols].bitcast(FP8X4),
+                lhsT_scale=w1_scale[:, cols],
+                rhs=xq_word[:, s0:s1].bitcast(FP8X4),
+                rhs_scale=xq_scale[:, s0:s1],
+                start=True,
+                stop=True,
+            )
+            nc.scalar.copy(y[t][:, s0:s1], acc[:])
+
+        w3_bf = keep.tile([P, N, PACK], BF16, name="w3_bf", tag="w_bf", align_bytes=64)
+        for half in range(2):
+            nc.gpsimd.tensor_scalar(
+                w3_bf[:, half * (N // 2) : (half + 1) * (N // 2), :],
+                w3_raw[half][:].rearrange("p j c -> p c j"),
+                1.0,
+                0.0,
+                ALU.mult,
+                ALU.add,
+            )
+
+        lf = [keep.tile([P, V], F32, name=f"lf{t}") for t in range(PACK)]
+        lo_a = reuse.tile([P, PACK, V], F32, name="lo_a", offset=3 * HALF_BYTES)
         for t in range(PACK):
-            for h in range(2):
-                nc.vector.tensor_copy(
-                    lf[t][:, h * 256 : (h + 1) * 256], y[t][:].indirect(left_sb[:, h * 16 : (h + 1) * 16])
-                )
-            for h in range(2):
+            nc.vector.tensor_copy(lf[t][:], y[t][:].indirect(left_sb[:]))
+        for t in range(POOL_TERMS):
+            nc.gpsimd.tensor_scalar(lo_a[:, t, :], lf[t][:], gl_twice_pool[:, t : t + 1], 0.0, ALU.mult, ALU.add)
+        for t in range(POOL_TERMS, PACK):
+            nc.scalar.activation(lo_a[:, t, :], lf[t][:], ACT.Copy, scale=gl_twice[:, t : t + 1])
+
+        lo_b = [keep.tile([P, PACK, HALF], F32, name=f"lo_b{h}") for h in range(2)]
+        hi_a = [keep.tile([P, PACK, HALF], F32, name=f"hi_a{h}") for h in range(2)]
+        hi_b = [keep.tile([P, PACK, HALF], F32, name=f"hi_b{h}") for h in range(2)]
+        for h in range(2):
+            cols = slice(h * HALF, (h + 1) * HALF)
+            dn = reuse.tile([P, PACK, HALF], F32, name=f"dn{h}", offset=h * HALF_BYTES)
+            for t in range(PACK):
+                one = slice(t, t + 1)
                 nc.vector.tensor_tensor(
-                    dn[t][:, h * 256 : (h + 1) * 256],
-                    y[t][:].indirect(right_sb[:, h * 16 : (h + 1) * 16]),
-                    lf[t][:, h * 256 : (h + 1) * 256],
-                    ALU.subtract,
+                    dn[:, t, :], y[t][:].indirect(right_sb[:, h * 16 : (h + 1) * 16]), lf[t][:, cols], ALU.subtract
                 )
-            scale_parts(t, 0)
-            if t == 0:
-                for c in range(1, len(CHUNKS)):
-                    scale_parts(t, c)
-            if t == 1:
-                w3_bf = interleave(w3_raw, "w3_bf", nc.scalar.copy)
-        w2_q = quantize(w2_bf, N, "w2")
-        for c in range(1, len(CHUNKS)):
-            for t in range(1, PACK):
-                scale_parts(t, c)
+                nc.scalar.activation(lo_b[h][:, t, :], dn[:, t, :], ACT.Copy, scale=gl_sb[:, one])
+                nc.scalar.activation(
+                    hi_a[h][:, t, :], dn[:, t, :], ACT.Relu, scale=slope_neg[:, one], bias=knee_neg[:, one]
+                )
+                nc.scalar.activation(
+                    hi_b[h][:, t, :], dn[:, t, :], ACT.Relu, scale=slope[:, one], bias=knee_neg[:, one]
+                )
+        w3_q = quantize(w3_bf[:].rearrange("p w j -> p (w j)"), N, "w3")
 
         def combine(first, second, op, n, name):
             grouped = keep.tile([P, n, PACK], BF16, name=name, align_bytes=64)
             nc.vector.tensor_tensor(
                 grouped[:].rearrange("p (c i) t -> p c t i", i=4),
-                first[:].rearrange("p t (c i) -> p c t i", i=4),
-                second[:].rearrange("p t (c i) -> p c t i", i=4),
+                first.rearrange("p t (c i) -> p c t i", i=4),
+                second.rearrange("p t (c i) -> p c t i", i=4),
                 op,
             )
-            return grouped
+            return grouped[:].rearrange("p w j -> p (w j)")
 
         def product(accs, w_q, act_q, first):
             for m in range(N // P):
@@ -213,12 +214,13 @@ def tile_picked_haarthr_none_p_kernel(
                 queue.dma_start(out[m * P : (m + 1) * P, v0 : v0 + n], res[:])
 
         for c, (v0, n) in enumerate(CHUNKS):
-            z_bf = combine(parts["lo_a", c], parts["lo_b", c], ALU.add, n, f"z_bf{c}")
-            if c == 0:
-                w3_q = quantize(w3_bf, N, "w3")
-            else:
+            h, part = v0 // HALF, slice(v0 % HALF, v0 % HALF + n)
+            z_bf = combine(lo_a[:, :, v0 : v0 + n], lo_b[h][:, :, part], ALU.add, n, f"z_bf{c}")
+            if c > 0:
                 finish(c - 1, accs, z2_bf)
-            accs = [psum.tile([P, n], F32, name="acc") for m in range(N // P)]
+            accs = [
+                psum.tile([P, n], F32, name=f"out_acc{c}_{m}", tag=f"bank{(4 * c + m) % 8}") for m in range(N // P)
+            ]
             product(accs, w2_q, quantize(z_bf, n, f"z{c}"), True)
-            z2_bf = combine(parts["hi_a", c], parts["hi_b", c], ALU.subtract, n, f"z2_bf{c}")
+            z2_bf = combine(hi_a[h][:, :, part], hi_b[h][:, :, part], ALU.subtract, n, f"z2_bf{c}")
         finish(len(CHUNKS) - 1, accs, z2_bf)

@@ -21,7 +21,7 @@ BANK = 512
 HALF = V // 2
 HALF_BYTES = PACK * HALF * 4
 X_HEAD = 640
-POOL_TERMS = 2
+POOL_TERMS = 3
 CHUNKS = ((0, 256), (256, 128), (384, 128))
 
 
@@ -48,10 +48,7 @@ def tile_picked_haarthr_none_p_kernel(
 
         w2_raw = [keep.tile([P, PACK, N // 2], F32, name=f"w2_raw{half}", tag=f"w2_then_y{half}") for half in range(2)]
         w2_rows = w2.rearrange("(p j) c -> p j c", j=PACK)
-        w3_raw = [
-            keep.tile([P, PACK, N // 2], F32, name=f"w3_raw{half}") for half in range(2)
-        ]
-        w3_rows = w3.rearrange("(p j) c -> p j c", j=PACK)
+        w3_raw = keep.tile([P, PACK, N], F32, name="w3_raw")
         x_rows = x_words[0].rearrange("p c r -> p (c r)").bitcast(I32)
 
         nc.vector.memset(x_scale_sb[:].bitcast(I32), 0)
@@ -68,8 +65,7 @@ def tile_picked_haarthr_none_p_kernel(
         nc.sync.dma_start(left_sb[:], left)
         for half in range(2):
             nc.sync.dma_start(w2_raw[half][:], w2_rows[:, :, half * (N // 2) : (half + 1) * (N // 2)])
-        for half in range(2):
-            nc.sync.dma_start(w3_raw[half][:], w3_rows[:, :, half * (N // 2) : (half + 1) * (N // 2)])
+        nc.sync.dma_start(w3_raw[:], w3.rearrange("(p j) c -> p j c", j=PACK))
         nc.sync.dma_start(right_sb[:], right)
 
         xq_scale = keep.tile([P, S], U8, name="xq_scale", align_bytes=64)
@@ -84,7 +80,7 @@ def tile_picked_haarthr_none_p_kernel(
                 w1_raw[half][:].rearrange("p j (m t) -> p m j t", t=PACK),
             )
         gl_twice = keep.tile([P, PACK], F32, name="gl_twice")
-        gl_twice_pool = reuse.tile([P, 16], F32, name="gl_twice_pool", offset=HALF_BYTES - 32)
+        gl_twice_pool = reuse.tile([P, 16], F32, name="gl_twice_pool", offset=2 * HALF_BYTES - 32)
         slope = keep.tile([P, PACK], F32, name="slope")
         slope_neg = keep.tile([P, PACK], F32, name="slope_neg")
         knee = keep.tile([P, PACK], F32, name="knee")
@@ -112,7 +108,7 @@ def tile_picked_haarthr_none_p_kernel(
             nc.vector.quantize_mx(out=word[:].bitcast(FP8X4), scales=scale[:], in_=grouped)
             return word, scale
 
-        w2_bf = keep.tile([P, N, PACK], BF16, name="w2_bf", tag="w_bf", align_bytes=64)
+        w2_bf = keep.tile([P, N, PACK], BF16, name="w2_bf", align_bytes=64)
         for half, copy in enumerate((nc.scalar.copy, nc.vector.tensor_copy)):
             copy(
                 w2_bf[:, half * (N // 2) : (half + 1) * (N // 2), :].rearrange("p (c i) j -> p c j i", i=4),
@@ -137,19 +133,13 @@ def tile_picked_haarthr_none_p_kernel(
             )
             nc.scalar.copy(y[t][:, s0:s1], acc[:])
 
-        w3_bf = keep.tile([P, N, PACK], BF16, name="w3_bf", tag="w_bf", align_bytes=64)
-        for half in range(2):
-            nc.gpsimd.tensor_scalar(
-                w3_bf[:, half * (N // 2) : (half + 1) * (N // 2), :],
-                w3_raw[half][:].rearrange("p j c -> p c j"),
-                1.0,
-                0.0,
-                ALU.mult,
-                ALU.add,
-            )
+        w3_bf = reuse.tile([P, N, PACK], BF16, name="w3_bf", align_bytes=64, offset=3 * HALF_BYTES)
+        nc.scalar.copy(
+            w3_bf[:].rearrange("p (c i) j -> p c j i", i=4), w3_raw[:].rearrange("p j (c i) -> p c j i", i=4)
+        )
 
         lf = [keep.tile([P, V], F32, name=f"lf{t}") for t in range(PACK)]
-        lo_a = reuse.tile([P, PACK, V], F32, name="lo_a", offset=3 * HALF_BYTES)
+        lo_a = keep.tile([P, PACK, V], F32, name="lo_a")
         for t in range(PACK):
             nc.vector.tensor_copy(lf[t][:], y[t][:].indirect(left_sb[:]))
         for t in range(POOL_TERMS):
@@ -157,25 +147,33 @@ def tile_picked_haarthr_none_p_kernel(
         for t in range(POOL_TERMS, PACK):
             nc.scalar.activation(lo_a[:, t, :], lf[t][:], ACT.Copy, scale=gl_twice[:, t : t + 1])
 
+        dn_all = reuse.tile([P, 2, PACK, HALF], F32, name="dn_all", offset=0)
         lo_b = [keep.tile([P, PACK, HALF], F32, name=f"lo_b{h}") for h in range(2)]
         hi_a = [keep.tile([P, PACK, HALF], F32, name=f"hi_a{h}") for h in range(2)]
         hi_b = [keep.tile([P, PACK, HALF], F32, name=f"hi_b{h}") for h in range(2)]
         for h in range(2):
             cols = slice(h * HALF, (h + 1) * HALF)
-            dn = reuse.tile([P, PACK, HALF], F32, name=f"dn{h}", offset=h * HALF_BYTES)
+            dn = dn_all[:, h]
             for t in range(PACK):
                 one = slice(t, t + 1)
                 nc.vector.tensor_tensor(
                     dn[:, t, :], y[t][:].indirect(right_sb[:, h * 16 : (h + 1) * 16]), lf[t][:, cols], ALU.subtract
                 )
-                nc.scalar.activation(lo_b[h][:, t, :], dn[:, t, :], ACT.Copy, scale=gl_sb[:, one])
-                nc.scalar.activation(
-                    hi_a[h][:, t, :], dn[:, t, :], ACT.Relu, scale=slope_neg[:, one], bias=knee_neg[:, one]
-                )
-                nc.scalar.activation(
-                    hi_b[h][:, t, :], dn[:, t, :], ACT.Relu, scale=slope[:, one], bias=knee_neg[:, one]
-                )
-        w3_q = quantize(w3_bf[:].rearrange("p w j -> p (w j)"), N, "w3")
+                last = (h, t) == (1, PACK - 1)
+                for part in (slice(0, P), slice(P, HALF)) if last else (slice(0, HALF),):
+                    nc.scalar.activation(lo_b[h][:, t, part], dn[:, t, part], ACT.Copy, scale=gl_sb[:, one])
+                    nc.scalar.activation(
+                        hi_a[h][:, t, part], dn[:, t, part], ACT.Relu, scale=slope_neg[:, one], bias=knee_neg[:, one]
+                    )
+                    nc.scalar.activation(
+                        hi_b[h][:, t, part], dn[:, t, part], ACT.Relu, scale=slope[:, one], bias=knee_neg[:, one]
+                    )
+        w3_word = reuse.tile([P, N], U32, name="w3_word", align_bytes=64, offset=2 * HALF_BYTES)
+        w3_scale = keep.tile([P, N], U8, name="w3_scale", align_bytes=64)
+        nc.vector.quantize_mx(
+            out=w3_word[:].bitcast(FP8X4), scales=w3_scale[:], in_=w3_bf[:].rearrange("p w j -> p (w j)")
+        )
+        w3_q = (w3_word, w3_scale)
 
         def combine(first, second, op, n, name):
             grouped = keep.tile([P, n, PACK], BF16, name=name, align_bytes=64)

@@ -22,6 +22,8 @@ HALF = V // 2
 HALF_BYTES = PACK * HALF * 4
 X_HEAD = 640
 POOL_TERMS = 3
+S_HEAD = 768
+W2_SCALAR = 192
 CHUNKS = ((0, 256), (256, 128), (384, 128))
 
 
@@ -46,7 +48,11 @@ def tile_picked_haarthr_none_p_kernel(
         w1_raw = [keep.tile([P, PACK, H // 2], F32, name=f"w1_raw{half}") for half in range(2)]
         w1_rows = w1.rearrange("(p j) c -> p j c", j=PACK)
 
-        w2_raw = [keep.tile([P, PACK, N // 2], F32, name=f"w2_raw{half}", tag=f"w2_then_y{half}") for half in range(2)]
+        w2_cols = (slice(0, W2_SCALAR), slice(W2_SCALAR, N))
+        w2_raw = [
+            keep.tile([P, PACK, cols.stop - cols.start], F32, name=f"w2_raw{part}", tag=f"w2_then_y{part}")
+            for part, cols in enumerate(w2_cols)
+        ]
         w2_rows = w2.rearrange("(p j) c -> p j c", j=PACK)
         w3_raw = keep.tile([P, PACK, N], F32, name="w3_raw")
         x_rows = x_words[0].rearrange("p c r -> p (c r)").bitcast(I32)
@@ -63,22 +69,26 @@ def tile_picked_haarthr_none_p_kernel(
             nc.sync.dma_start(w1_raw[half][:], w1_rows[:, :, half * (H // 2) : (half + 1) * (H // 2)])
         nc.sync.dma_start(gl_sb[:], gl.rearrange("(p t) o -> p (t o)", t=PACK))
         nc.sync.dma_start(left_sb[:], left)
-        for half in range(2):
-            nc.sync.dma_start(w2_raw[half][:], w2_rows[:, :, half * (N // 2) : (half + 1) * (N // 2)])
+        for part, cols in enumerate(w2_cols):
+            nc.sync.dma_start(w2_raw[part][:], w2_rows[:, :, cols])
         nc.sync.dma_start(w3_raw[:], w3.rearrange("(p j) c -> p j c", j=PACK))
         nc.sync.dma_start(right_sb[:], right)
 
         xq_scale = keep.tile([P, S], U8, name="xq_scale", align_bytes=64)
-        xq_word = keep.tile([P, S], U32, name="xq_word", align_bytes=64)
+        xq_head = keep.tile([P, S_HEAD], U32, name="xq_head", align_bytes=64)
         nc.vector.tensor_copy(xq_scale[:], x_scale_sb[:].indirect(offs_sb[:]))
-        nc.vector.tensor_copy(xq_word[:], x_word_sb[:].indirect(offs_sb[:]))
+        nc.vector.tensor_copy(xq_head[:], x_word_sb[:].indirect(offs_sb[:, : S_HEAD // 16]))
 
-        w1_bf = keep.tile([P, PACK, P, PACK], BF16, name="w1_bf", align_bytes=64)
+        w1_bf = [
+            keep.tile([P, 2, P, PACK], BF16, name=f"w1_bf{pair}", tag=f"w1_bf{pair}", align_bytes=64)
+            for pair in range(2)
+        ]
         for half in range(2):
-            nc.scalar.copy(
-                w1_bf[:, :, half * (P // 2) : (half + 1) * (P // 2), :].rearrange("p t m j -> p m j t"),
-                w1_raw[half][:].rearrange("p j (m t) -> p m j t", t=PACK),
-            )
+            for pair in range(2):
+                nc.scalar.copy(
+                    w1_bf[pair][:, :, half * (P // 2) : (half + 1) * (P // 2), :].rearrange("p t m j -> p m j t"),
+                    w1_raw[half][:].rearrange("p j (m t) -> p m j t", t=PACK)[:, :, :, 2 * pair : 2 * pair + 2],
+                )
         gl_twice = keep.tile([P, PACK], F32, name="gl_twice")
         gl_twice_pool = reuse.tile([P, 16], F32, name="gl_twice_pool", offset=2 * HALF_BYTES - 32)
         slope = keep.tile([P, PACK], F32, name="slope")
@@ -94,13 +104,16 @@ def tile_picked_haarthr_none_p_kernel(
 
         w1_word = reuse.tile([P, H], U32, name="w1_word", align_bytes=64, offset=3 * HALF_BYTES)
         w1_scale = keep.tile([P, H], U8, name="w1_scale", align_bytes=64)
-        for t0, t1 in ((0, 1), (1, 2), (2, 4)):
-            cols = slice(t0 * P, t1 * P)
+        xq_tail = keep.tile([P, S - S_HEAD], U32, name="xq_tail", tag="w1_bf0", align_bytes=64)
+        for pair in range(2):
+            cols = slice(2 * pair * P, (2 * pair + 2) * P)
             nc.vector.quantize_mx(
                 out=w1_word[:, cols].bitcast(FP8X4),
                 scales=w1_scale[:, cols],
-                in_=w1_bf[:, t0:t1].rearrange("p t m j -> p (t m j)"),
+                in_=w1_bf[pair][:].rearrange("p t m j -> p (t m j)"),
             )
+            if pair == 0:
+                nc.vector.tensor_copy(xq_tail[:], x_word_sb[:].indirect(offs_sb[:, S_HEAD // 16 :]))
 
         def quantize(grouped, width, name):
             word = keep.tile([P, width], U32, name=f"{name}_word", align_bytes=64)
@@ -111,7 +124,7 @@ def tile_picked_haarthr_none_p_kernel(
         w2_bf = keep.tile([P, N, PACK], BF16, name="w2_bf", align_bytes=64)
         for half, copy in enumerate((nc.scalar.copy, nc.vector.tensor_copy)):
             copy(
-                w2_bf[:, half * (N // 2) : (half + 1) * (N // 2), :].rearrange("p (c i) j -> p c j i", i=4),
+                w2_bf[:, w2_cols[half], :].rearrange("p (c i) j -> p c j i", i=4),
                 w2_raw[half][:].rearrange("p j (c i) -> p c j i", i=4),
             )
         w2_q = quantize(w2_bf[:].rearrange("p w j -> p (w j)"), N, "w2")
@@ -122,15 +135,18 @@ def tile_picked_haarthr_none_p_kernel(
         for step, (t, s0, s1) in enumerate(steps):
             cols = slice(t * P, (t + 1) * P)
             acc = psum.tile([P, s1 - s0], F32, name=f"y_acc{step}", tag=f"bank{step % 4}")
-            nc.tensor.matmul_mx(
-                out=acc[:],
-                lhsT=w1_word[:, cols].bitcast(FP8X4),
-                lhsT_scale=w1_scale[:, cols],
-                rhs=xq_word[:, s0:s1].bitcast(FP8X4),
-                rhs_scale=xq_scale[:, s0:s1],
-                start=True,
-                stop=True,
-            )
+            cuts = (s0, S_HEAD, s1) if s0 < S_HEAD < s1 else (s0, s1)
+            for a, b in zip(cuts[:-1], cuts[1:]):
+                words = xq_head[:, a:b] if b <= S_HEAD else xq_tail[:, a - S_HEAD : b - S_HEAD]
+                nc.tensor.matmul_mx(
+                    out=acc[:, a - s0 : b - s0],
+                    lhsT=w1_word[:, cols].bitcast(FP8X4),
+                    lhsT_scale=w1_scale[:, cols],
+                    rhs=words.bitcast(FP8X4),
+                    rhs_scale=xq_scale[:, a:b],
+                    start=True,
+                    stop=True,
+                )
             nc.scalar.copy(y[t][:, s0:s1], acc[:])
 
         w3_bf = reuse.tile([P, N, PACK], BF16, name="w3_bf", align_bytes=64, offset=3 * HALF_BYTES)

@@ -59,7 +59,7 @@ def tile_picked_haarthr_none_p_kernel(
 
         nc.vector.memset(x_scale_sb[:].bitcast(I32), 0)
         nc.sync.dma_start(x_word_sb[:, :X_HEAD].bitcast(I32), x_rows[:, :X_HEAD])
-        nc.sync.dma_start(gh_sb[:], gh.rearrange("(p t) o -> p (t o)", t=PACK))
+        nc.sync.dma_start(gl_sb[:], gl.rearrange("(p t) o -> p (t o)", t=PACK))
         for q in range(4):
             nc.sync.dma_start(
                 x_scale_sb[32 * q : 32 * q + 4, :].bitcast(I32), x_scales[0, 4 * q : 4 * q + 4, :].bitcast(I32)
@@ -67,10 +67,10 @@ def tile_picked_haarthr_none_p_kernel(
         nc.sync.dma_start(x_word_sb[:, X_HEAD:].bitcast(I32), x_rows[:, X_HEAD:])
         for half in range(2):
             nc.sync.dma_start(w1_raw[half][:], w1_rows[:, :, half * (H // 2) : (half + 1) * (H // 2)])
-        nc.sync.dma_start(gl_sb[:], gl.rearrange("(p t) o -> p (t o)", t=PACK))
-        nc.sync.dma_start(left_sb[:], left)
         for part, cols in enumerate(w2_cols):
             nc.sync.dma_start(w2_raw[part][:], w2_rows[:, :, cols])
+        nc.sync.dma_start(left_sb[:], left)
+        nc.sync.dma_start(gh_sb[:], gh.rearrange("(p t) o -> p (t o)", t=PACK))
         nc.sync.dma_start(w3_raw[:], w3.rearrange("(p j) c -> p j c", j=PACK))
         nc.sync.dma_start(right_sb[:], right)
 
@@ -91,19 +91,11 @@ def tile_picked_haarthr_none_p_kernel(
                 )
         gl_twice = keep.tile([P, PACK], F32, name="gl_twice")
         gl_twice_pool = reuse.tile([P, 16], F32, name="gl_twice_pool", offset=2 * HALF_BYTES - 32)
-        slope = keep.tile([P, PACK], F32, name="slope")
-        slope_neg = keep.tile([P, PACK], F32, name="slope_neg")
-        knee = keep.tile([P, PACK], F32, name="knee")
-        knee_neg = keep.tile([P, PACK], F32, name="knee_neg")
         nc.scalar.activation(gl_twice[:], gl_sb[:], ACT.Copy, scale=2.0)
         nc.scalar.activation(gl_twice_pool[:, :PACK], gl_sb[:], ACT.Copy, scale=2.0)
-        nc.scalar.activation(slope[:], gh_sb[:], ACT.Copy, scale=0.75)
-        nc.scalar.activation(slope_neg[:], gh_sb[:], ACT.Copy, scale=-0.75)
-        nc.scalar.activation(knee[:], gh_sb[:], ACT.Abs, scale=0.5)
-        nc.scalar.activation(knee_neg[:], knee[:], ACT.Copy, scale=-1.0)
 
         w1_word = reuse.tile([P, H], U32, name="w1_word", align_bytes=64, offset=3 * HALF_BYTES)
-        w1_scale = keep.tile([P, H], U8, name="w1_scale", align_bytes=64)
+        w1_scale = reuse.tile([P, H], U8, name="w1_scale", align_bytes=64, offset=4 * HALF_BYTES)
         xq_tail = keep.tile([P, S - S_HEAD], U32, name="xq_tail", tag="w1_bf0", align_bytes=64)
         for pair in range(2):
             cols = slice(2 * pair * P, (2 * pair + 2) * P)
@@ -148,6 +140,15 @@ def tile_picked_haarthr_none_p_kernel(
                     stop=True,
                 )
             nc.scalar.copy(y[t][:, s0:s1], acc[:])
+
+        slope, slope_neg, knee, knee_neg = (
+            reuse.tile([P, PACK], F32, name=name, offset=4 * HALF_BYTES + 32 * k)
+            for k, name in enumerate(("slope", "slope_neg", "knee", "knee_neg"))
+        )
+        nc.scalar.activation(slope[:], gh_sb[:], ACT.Copy, scale=0.75)
+        nc.scalar.activation(slope_neg[:], gh_sb[:], ACT.Copy, scale=-0.75)
+        nc.scalar.activation(knee[:], gh_sb[:], ACT.Abs, scale=0.5)
+        nc.scalar.activation(knee_neg[:], knee[:], ACT.Copy, scale=-1.0)
 
         w3_bf = reuse.tile([P, N, PACK], BF16, name="w3_bf", align_bytes=64, offset=3 * HALF_BYTES)
         nc.scalar.copy(

@@ -166,8 +166,17 @@ def tile_picked_haarthr_none_p_kernel(
 
         dn_all = reuse.tile([P, 2, PACK, HALF], F32, name="dn_all", offset=0)
         lo_b = [keep.tile([P, PACK, HALF], F32, name=f"lo_b{h}") for h in range(2)]
-        hi_a = [keep.tile([P, PACK, HALF], F32, name=f"hi_a{h}") for h in range(2)]
-        hi_b = [keep.tile([P, PACK, HALF], F32, name=f"hi_b{h}") for h in range(2)]
+        hi_a, hi_b = (
+            [
+                keep.tile([P, 2, HALF, 2], BF16, name=f"{name}0"),
+                keep.tile([P, PACK, HALF], F32, name=f"{name}1"),
+            ]
+            for name in ("hi_a", "hi_b")
+        )
+
+        def term(hi, h, t, part):
+            return hi[h][:, t // 2, part, t % 2] if h == 0 else hi[h][:, t, part]
+
         for h in range(2):
             cols = slice(h * HALF, (h + 1) * HALF)
             dn = dn_all[:, h]
@@ -180,10 +189,10 @@ def tile_picked_haarthr_none_p_kernel(
                 for part in (slice(0, P), slice(P, HALF)) if last else (slice(0, HALF),):
                     nc.scalar.activation(lo_b[h][:, t, part], dn[:, t, part], ACT.Copy, scale=gl_sb[:, one])
                     nc.scalar.activation(
-                        hi_a[h][:, t, part], dn[:, t, part], ACT.Relu, scale=slope_neg[:, one], bias=knee_neg[:, one]
+                        term(hi_a, h, t, part), dn[:, t, part], ACT.Relu, scale=slope_neg[:, one], bias=knee_neg[:, one]
                     )
                     nc.scalar.activation(
-                        hi_b[h][:, t, part], dn[:, t, part], ACT.Relu, scale=slope[:, one], bias=knee_neg[:, one]
+                        term(hi_b, h, t, part), dn[:, t, part], ACT.Relu, scale=slope[:, one], bias=knee_neg[:, one]
                     )
         w3_word = reuse.tile([P, N], U32, name="w3_word", align_bytes=64, offset=2 * HALF_BYTES)
         w3_scale = keep.tile([P, N], U8, name="w3_scale", align_bytes=64)
@@ -237,5 +246,15 @@ def tile_picked_haarthr_none_p_kernel(
                 psum.tile([P, n], F32, name=f"out_acc{c}_{m}", tag=f"bank{(4 * c + m) % 8}") for m in range(N // P)
             ]
             product(accs, w2_q, quantize(z_bf, n, f"z{c}"), True)
-            z2_bf = combine(hi_a[h][:, :, part], hi_b[h][:, :, part], ALU.subtract, n, f"z2_bf{c}")
+            if h == 0:
+                grouped = keep.tile([P, n, PACK], BF16, name=f"z2_bf{c}", align_bytes=64)
+                nc.vector.tensor_tensor(
+                    grouped[:].rearrange("p v (u e) -> p v u e", e=2),
+                    hi_a[h][:].rearrange("p u v e -> p v u e"),
+                    hi_b[h][:].rearrange("p u v e -> p v u e"),
+                    ALU.subtract,
+                )
+                z2_bf = grouped[:].rearrange("p w j -> p (w j)")
+            else:
+                z2_bf = combine(hi_a[h][:, :, part], hi_b[h][:, :, part], ALU.subtract, n, f"z2_bf{c}")
         finish(len(CHUNKS) - 1, accs, z2_bf)

@@ -21,9 +21,9 @@ BANK = 512
 HALF = V // 2
 HALF_BYTES = PACK * HALF * 4
 X_HEAD = 640
-POOL_TERMS = 3
 S_HEAD = 768
-W2_SCALAR = 192
+W1_HEAD = 256
+TINY = 2.0**-80
 CHUNKS = ((0, 256), (256, 128), (384, 128))
 
 
@@ -45,16 +45,15 @@ def tile_picked_haarthr_none_p_kernel(
         x_word_sb = keep.tile([P, T], U32, name="x_word_sb", align_bytes=64)
         gl_sb = keep.tile([P, PACK], F32, name="gl_sb")
         gh_sb = keep.tile([P, PACK], F32, name="gh_sb")
-        w1_raw = [keep.tile([P, PACK, H // 2], F32, name=f"w1_raw{half}") for half in range(2)]
-        w1_rows = w1.rearrange("(p j) c -> p j c", j=PACK)
-
-        w2_cols = (slice(0, W2_SCALAR), slice(W2_SCALAR, N))
-        w2_raw = [
-            keep.tile([P, PACK, cols.stop - cols.start], F32, name=f"w2_raw{part}", tag=f"w2_then_y{part}")
-            for part, cols in enumerate(w2_cols)
+        w1_cols = (slice(0, W1_HEAD), slice(W1_HEAD, H))
+        w1_raw = [
+            keep.tile([P, PACK, cols.stop - cols.start], F32, name=f"w1_raw{part}") for part, cols in enumerate(w1_cols)
         ]
+        w1_rows = w1.rearrange("(p j) c -> p j c", j=PACK)
+        w2_raw = [keep.tile([P, PACK, N // 2], F32, name=f"w2_raw{half}", tag=f"w2_then_y{half}") for half in range(2)]
         w2_rows = w2.rearrange("(p j) c -> p j c", j=PACK)
-        w3_raw = keep.tile([P, PACK, N], F32, name="w3_raw")
+        w3_then_dn = keep.tile([P, PACK * N], F32, name="w3_then_dn")
+        w3_raw = w3_then_dn[:].rearrange("p (j c) -> p j c", j=PACK)
         x_rows = x_words[0].rearrange("p c r -> p (c r)").bitcast(I32)
 
         nc.vector.memset(x_scale_sb[:].bitcast(I32), 0)
@@ -65,37 +64,42 @@ def tile_picked_haarthr_none_p_kernel(
                 x_scale_sb[32 * q : 32 * q + 4, :].bitcast(I32), x_scales[0, 4 * q : 4 * q + 4, :].bitcast(I32)
             )
         nc.sync.dma_start(x_word_sb[:, X_HEAD:].bitcast(I32), x_rows[:, X_HEAD:])
-        for half in range(2):
-            nc.sync.dma_start(w1_raw[half][:], w1_rows[:, :, half * (H // 2) : (half + 1) * (H // 2)])
-        for part, cols in enumerate(w2_cols):
-            nc.sync.dma_start(w2_raw[part][:], w2_rows[:, :, cols])
-        nc.sync.dma_start(left_sb[:], left)
+        for part, cols in enumerate(w1_cols):
+            nc.sync.dma_start(w1_raw[part][:], w1_rows[:, :, cols])
         nc.sync.dma_start(gh_sb[:], gh.rearrange("(p t) o -> p (t o)", t=PACK))
-        nc.sync.dma_start(w3_raw[:], w3.rearrange("(p j) c -> p j c", j=PACK))
+        nc.sync.dma_start(w2_raw[0][:], w2_rows[:, :, : N // 2])
+        nc.sync.dma_start(left_sb[:], left)
         nc.sync.dma_start(right_sb[:], right)
+        nc.sync.dma_start(w2_raw[1][:], w2_rows[:, :, N // 2 :])
+        nc.sync.dma_start(w3_raw, w3.rearrange("(p j) c -> p j c", j=PACK))
 
         xq_scale = keep.tile([P, S], U8, name="xq_scale", align_bytes=64)
         xq_head = keep.tile([P, S_HEAD], U32, name="xq_head", align_bytes=64)
         nc.vector.tensor_copy(xq_scale[:], x_scale_sb[:].indirect(offs_sb[:]))
         nc.vector.tensor_copy(xq_head[:], x_word_sb[:].indirect(offs_sb[:, : S_HEAD // 16]))
 
+        gl_abs = keep.tile([P, PACK], F32, name="gl_abs")
+        gl_lift = keep.tile([P, PACK], F32, name="gl_lift")
+        gain = reuse.tile([P, PACK], F32, name="gain", offset=0)
+        gain_last = reuse.tile([P, 1], F32, name="gain_last", offset=2 * HALF_BYTES)
+        nc.scalar.activation(gl_abs[:], gl_sb[:], ACT.Abs)
+        nc.gpsimd.tensor_scalar(gl_lift[:], gl_abs[:], TINY, 2.0 * TINY, ALU.is_lt, ALU.mult)
+        nc.gpsimd.tensor_tensor(gain[:], gl_sb[:], gl_lift[:], ALU.add)
+        nc.gpsimd.tensor_tensor(gain_last[:], gl_sb[:, PACK - 1 :], gl_lift[:, PACK - 1 :], ALU.add)
+
         w1_bf = [
             keep.tile([P, 2, P, PACK], BF16, name=f"w1_bf{pair}", tag=f"w1_bf{pair}", align_bytes=64)
             for pair in range(2)
         ]
-        for half in range(2):
+        for part, cols in enumerate(w1_cols):
             for pair in range(2):
                 nc.scalar.copy(
-                    w1_bf[pair][:, :, half * (P // 2) : (half + 1) * (P // 2), :].rearrange("p t m j -> p m j t"),
-                    w1_raw[half][:].rearrange("p j (m t) -> p m j t", t=PACK)[:, :, :, 2 * pair : 2 * pair + 2],
+                    w1_bf[pair][:, :, cols.start // PACK : cols.stop // PACK, :].rearrange("p t m j -> p m j t"),
+                    w1_raw[part][:].rearrange("p j (m t) -> p m j t", t=PACK)[:, :, :, 2 * pair : 2 * pair + 2],
                 )
-        gl_twice = keep.tile([P, PACK], F32, name="gl_twice")
-        gl_twice_pool = reuse.tile([P, 16], F32, name="gl_twice_pool", offset=2 * HALF_BYTES - 32)
-        nc.scalar.activation(gl_twice[:], gl_sb[:], ACT.Copy, scale=2.0)
-        nc.scalar.activation(gl_twice_pool[:, :PACK], gl_sb[:], ACT.Copy, scale=2.0)
 
-        w1_word = reuse.tile([P, H], U32, name="w1_word", align_bytes=64, offset=3 * HALF_BYTES)
-        w1_scale = reuse.tile([P, H], U8, name="w1_scale", align_bytes=64, offset=4 * HALF_BYTES)
+        w1_word = keep.tile([P, H], U32, name="w1_word", align_bytes=64)
+        w1_scale = keep.tile([P, H], U8, name="w1_scale", align_bytes=64)
         xq_tail = keep.tile([P, S - S_HEAD], U32, name="xq_tail", tag="w1_bf0", align_bytes=64)
         for pair in range(2):
             cols = slice(2 * pair * P, (2 * pair + 2) * P)
@@ -106,6 +110,15 @@ def tile_picked_haarthr_none_p_kernel(
             )
             if pair == 0:
                 nc.vector.tensor_copy(xq_tail[:], x_word_sb[:].indirect(offs_sb[:, S_HEAD // 16 :]))
+        gain_inv = keep.tile([P, PACK], F32, name="gain_inv")
+        slope, slope_neg, knee, knee_neg = (
+            keep.tile([P, PACK], F32, name=name) for name in ("slope", "slope_neg", "knee", "knee_neg")
+        )
+        nc.vector.reciprocal(gain_inv[:], gain[:])
+        nc.vector.scalar_tensor_tensor(slope[:], gain_inv[:], 0.75, gh_sb[:], ALU.mult, ALU.mult)
+        nc.scalar.activation(knee[:], gh_sb[:], ACT.Abs, scale=0.5)
+        nc.scalar.activation(knee_neg[:], knee[:], ACT.Copy, scale=-1.0)
+        nc.scalar.activation(slope_neg[:], slope[:], ACT.Copy, scale=-1.0)
 
         def quantize(grouped, width, name):
             word = keep.tile([P, width], U32, name=f"{name}_word", align_bytes=64)
@@ -113,22 +126,37 @@ def tile_picked_haarthr_none_p_kernel(
             nc.vector.quantize_mx(out=word[:].bitcast(FP8X4), scales=scale[:], in_=grouped)
             return word, scale
 
-        w2_bf = keep.tile([P, N, PACK], BF16, name="w2_bf", align_bytes=64)
-        for half, copy in enumerate((nc.scalar.copy, nc.vector.tensor_copy)):
-            copy(
-                w2_bf[:, w2_cols[half], :].rearrange("p (c i) j -> p c j i", i=4),
-                w2_raw[half][:].rearrange("p j (c i) -> p c j i", i=4),
+        def cast(dst, raw):
+            nc.vector.tensor_copy(
+                dst.rearrange("p (c i) j -> p c j i", i=4), raw.rearrange("p j (c i) -> p c j i", i=4)
             )
-        w2_q = quantize(w2_bf[:].rearrange("p w j -> p (w j)"), N, "w2")
 
-        y = [keep.tile([P, S], F32, name=f"y{t}", tag=f"w2_then_y{t}") for t in range(PACK)]
-        steps = [(0, s0, s0 + BANK // 2) for s0 in range(0, S, BANK // 2)]
-        steps = steps + [(t, s0, s0 + BANK) for t in range(1, PACK) for s0 in (0, BANK)]
-        for step, (t, s0, s1) in enumerate(steps):
+        y = [keep.tile([P, S], F32, name=f"y{t}", tag="w2_then_y0" if t == 1 else f"y{t}") for t in range(PACK)]
+        lf = [
+            keep.tile([P, PACK, HALF], F32, name="lf0"),
+            reuse.tile([P, PACK, HALF], F32, name="lf1", offset=2 * HALF_BYTES),
+        ]
+        dn = [
+            w3_raw[:, :, :HALF],
+            w3_raw[:, :, HALF:],
+        ]
+        hi = [
+            reuse.tile([P, 2, PACK, HALF], F32, name="hi0", offset=0),
+            keep.tile([P, 2, PACK, HALF], F32, name="hi1"),
+        ]
+        hi_a = [hi[h][:, 0] for h in range(2)]
+        hi_b = [hi[h][:, 1] for h in range(2)]
+
+        y_acc = {}
+        pieces = [(0, 0, BANK), (0, BANK, S_HEAD), (0, S_HEAD, S)]
+        pieces = pieces + [(t, s0, s0 + BANK) for s0 in (0, BANK) for t in (1, 2)]
+        pieces = pieces + [(3, s0, s0 + BANK) for s0 in (0, BANK)]
+        for step, (t, s0, s1) in enumerate(pieces):
             cols = slice(t * P, (t + 1) * P)
-            acc = psum.tile([P, s1 - s0], F32, name=f"y_acc{step}", tag=f"bank{step % 4}")
-            cuts = (s0, S_HEAD, s1) if s0 < S_HEAD < s1 else (s0, s1)
-            for a, b in zip(cuts[:-1], cuts[1:]):
+            acc = psum.tile([P, s1 - s0], F32, name=f"y_acc{t}_{s0}", tag=f"bank{step % 8}")
+            y_acc[t, s0] = acc
+            parts = (s0, S_HEAD, s1) if s0 < S_HEAD < s1 else (s0, s1)
+            for a, b in zip(parts[:-1], parts[1:]):
                 words = xq_head[:, a:b] if b <= S_HEAD else xq_tail[:, a - S_HEAD : b - S_HEAD]
                 nc.tensor.matmul_mx(
                     out=acc[:, a - s0 : b - s0],
@@ -139,122 +167,142 @@ def tile_picked_haarthr_none_p_kernel(
                     start=True,
                     stop=True,
                 )
-            nc.scalar.copy(y[t][:, s0:s1], acc[:])
 
-        slope, slope_neg, knee, knee_neg = (
-            reuse.tile([P, PACK], F32, name=name, offset=4 * HALF_BYTES + 32 * k)
-            for k, name in enumerate(("slope", "slope_neg", "knee", "knee_neg"))
-        )
-        nc.scalar.activation(slope[:], gh_sb[:], ACT.Copy, scale=0.75)
-        nc.scalar.activation(slope_neg[:], gh_sb[:], ACT.Copy, scale=-0.75)
-        nc.scalar.activation(knee[:], gh_sb[:], ACT.Abs, scale=0.5)
-        nc.scalar.activation(knee_neg[:], knee[:], ACT.Copy, scale=-1.0)
+        def copy_y(t, s0):
+            acc = y_acc[t, s0]
+            window = y[t][:, s0 : s0 + acc.shape[1]]
+            if t == 1:
+                nc.vector.tensor_scalar(window, acc[:], gain[:, t : t + 1], None, ALU.mult)
+            else:
+                factor = gain_last[:] if (t, s0) == (PACK - 1, BANK) else gain[:, t : t + 1]
+                nc.scalar.activation(window, acc[:], ACT.Copy, scale=factor)
 
-        w3_bf = reuse.tile([P, N, PACK], BF16, name="w3_bf", align_bytes=64, offset=3 * HALF_BYTES)
-        nc.scalar.copy(
-            w3_bf[:].rearrange("p (c i) j -> p c j i", i=4), w3_raw[:].rearrange("p j (c i) -> p c j i", i=4)
-        )
+        def fetch_left(h, t):
+            nc.scalar.activation(lf[h][:, t, :], y[t][:].indirect(left_sb[:, h * 16 : (h + 1) * 16]), ACT.Copy)
 
-        lf = [keep.tile([P, V], F32, name=f"lf{t}") for t in range(PACK)]
-        lo_a = keep.tile([P, PACK, V], F32, name="lo_a")
-        for t in range(PACK):
-            nc.vector.tensor_copy(lf[t][:], y[t][:].indirect(left_sb[:]))
-        for t in range(POOL_TERMS):
-            nc.gpsimd.tensor_scalar(lo_a[:, t, :], lf[t][:], gl_twice_pool[:, t : t + 1], 0.0, ALU.mult, ALU.add)
-        for t in range(POOL_TERMS, PACK):
-            nc.scalar.activation(lo_a[:, t, :], lf[t][:], ACT.Copy, scale=gl_twice[:, t : t + 1])
-
-        dn_all = reuse.tile([P, 2, PACK, HALF], F32, name="dn_all", offset=0)
-        lo_b = [keep.tile([P, PACK, HALF], F32, name=f"lo_b{h}") for h in range(2)]
-        hi_a, hi_b = (
-            [
-                keep.tile([P, 2, HALF, 2], BF16, name=f"{name}0"),
-                keep.tile([P, PACK, HALF], F32, name=f"{name}1"),
-            ]
-            for name in ("hi_a", "hi_b")
-        )
-
-        def term(hi, h, t, part):
-            return hi[h][:, t // 2, part, t % 2] if h == 0 else hi[h][:, t, part]
-
-        for h in range(2):
-            cols = slice(h * HALF, (h + 1) * HALF)
-            dn = dn_all[:, h]
-            for t in range(PACK):
-                one = slice(t, t + 1)
-                nc.vector.tensor_tensor(
-                    dn[:, t, :], y[t][:].indirect(right_sb[:, h * 16 : (h + 1) * 16]), lf[t][:, cols], ALU.subtract
-                )
-                last = (h, t) == (1, PACK - 1)
-                for part in (slice(0, P), slice(P, HALF)) if last else (slice(0, HALF),):
-                    nc.scalar.activation(lo_b[h][:, t, part], dn[:, t, part], ACT.Copy, scale=gl_sb[:, one])
-                    nc.scalar.activation(
-                        term(hi_a, h, t, part), dn[:, t, part], ACT.Relu, scale=slope_neg[:, one], bias=knee_neg[:, one]
-                    )
-                    nc.scalar.activation(
-                        term(hi_b, h, t, part), dn[:, t, part], ACT.Relu, scale=slope[:, one], bias=knee_neg[:, one]
-                    )
-        w3_word = reuse.tile([P, N], U32, name="w3_word", align_bytes=64, offset=2 * HALF_BYTES)
-        w3_scale = keep.tile([P, N], U8, name="w3_scale", align_bytes=64)
-        nc.vector.quantize_mx(
-            out=w3_word[:].bitcast(FP8X4), scales=w3_scale[:], in_=w3_bf[:].rearrange("p w j -> p (w j)")
-        )
-        w3_q = (w3_word, w3_scale)
-
-        def combine(first, second, op, n, name):
-            grouped = keep.tile([P, n, PACK], BF16, name=name, align_bytes=64)
+        def fetch_right(h, t):
             nc.vector.tensor_tensor(
-                grouped[:].rearrange("p (c i) t -> p c t i", i=4),
-                first.rearrange("p t (c i) -> p c t i", i=4),
-                second.rearrange("p t (c i) -> p c t i", i=4),
-                op,
+                dn[h][:, t, :], y[t][:].indirect(right_sb[:, h * 16 : (h + 1) * 16]), lf[h][:, t, :], ALU.subtract
+            )
+
+        def shrink_terms(h, t, part):
+            one = slice(t, t + 1)
+            nc.scalar.activation(
+                hi_a[h][:, t, part], dn[h][:, t, part], ACT.Relu, scale=slope_neg[:, one], bias=knee_neg[:, one]
+            )
+            nc.scalar.activation(
+                hi_b[h][:, t, part], dn[h][:, t, part], ACT.Relu, scale=slope[:, one], bias=knee_neg[:, one]
+            )
+
+        w23_bf = keep.tile([P, 2 * N, PACK], BF16, name="w23_bf", align_bytes=64)
+        w2_bf, w3_bf = w23_bf[:, :N, :], w23_bf[:, N:, :]
+        cast(w2_bf[:, : N // 2, :], w2_raw[0][:])
+        for s0 in (0, BANK, S_HEAD):
+            copy_y(0, s0)
+        copy_y(1, 0)
+        copy_y(1, BANK)
+        cast(w2_bf[:, N // 2 :, :], w2_raw[1][:])
+        copy_y(2, 0)
+        fetch_left(0, 0)
+        copy_y(2, BANK)
+        for half in range(2):
+            cols = slice(half * (N // 2), (half + 1) * (N // 2))
+            cast(w3_bf[:, cols, :], w3_raw[:, :, cols])
+        fetch_right(0, 0)
+        w23_word, w23_scale = quantize(w23_bf[:].rearrange("p w j -> p (w j)"), 2 * N, "w23")
+        w2_q, w3_q = (w23_word[:, :N], w23_scale[:, :N]), (w23_word[:, N:], w23_scale[:, N:])
+        copy_y(3, 0)
+        fetch_left(0, 1)
+        fetch_right(0, 1)
+        copy_y(3, BANK)
+        for t in (2, 3):
+            fetch_left(0, t)
+            fetch_right(0, t)
+
+        def join_low(h):
+            grouped = keep.tile([P, HALF, PACK], BF16, name=f"z_bf{h}", align_bytes=64)
+            nc.vector.scalar_tensor_tensor(
+                grouped[:],
+                lf[h][:].rearrange("p t c -> p c t"),
+                2.0,
+                dn[h].rearrange("p t c -> p c t"),
+                ALU.mult,
+                ALU.add,
             )
             return grouped[:].rearrange("p w j -> p (w j)")
 
-        def product(accs, w_q, act_q, first):
+        def join_high(c):
+            v0, n = CHUNKS[c]
+            h, part = v0 // HALF, slice(v0 % HALF, v0 % HALF + n)
+            grouped = keep.tile([P, n, PACK], BF16, name=f"z2_bf{c}", align_bytes=64)
+            nc.vector.tensor_tensor(
+                grouped[:].rearrange("p (c i) t -> p c t i", i=4),
+                hi_a[h][:, :, part].rearrange("p t (c i) -> p c t i", i=4),
+                hi_b[h][:, :, part].rearrange("p t (c i) -> p c t i", i=4),
+                ALU.subtract,
+            )
+            return grouped[:].rearrange("p w j -> p (w j)")
+
+        out_rows = out.rearrange("(m p) v -> p m v", p=P)
+        BANKS = ((0, 1), (2,), (3, 4))
+
+        def open_sums(c):
+            n = CHUNKS[c][1]
+            share = (N // P) // len(BANKS[c])
+            return [psum.tile([P, share, n], F32, name=f"out_acc{c}_{b}", tag=f"bank{b}") for b in BANKS[c]]
+
+        def product(accs, w_q, act_q, first, part=slice(None)):
+            share = (N // P) // len(accs)
             for m in range(N // P):
                 cols = slice(m * P, (m + 1) * P)
                 nc.tensor.matmul_mx(
-                    out=accs[m][:],
+                    out=accs[m // share][:, m % share, :],
                     lhsT=w_q[0][:, cols].bitcast(FP8X4),
                     lhsT_scale=w_q[1][:, cols],
-                    rhs=act_q[0][:].bitcast(FP8X4),
-                    rhs_scale=act_q[1][:],
-                    start=first,
-                    stop=not first,
+                    rhs=act_q[0][:, part].bitcast(FP8X4),
+                    rhs_scale=act_q[1][:, part],
+                    start=first and m % share == 0,
+                    stop=not first and m % share == share - 1,
                 )
 
-        def finish(c, accs, z2_bf):
+        def store(c, accs):
             v0, n = CHUNKS[c]
-            product(accs, w3_q, quantize(z2_bf, n, f"z2{c}"), False)
+            share = (N // P) // len(accs)
             last = c == len(CHUNKS) - 1
-            for m in range(N // P):
-                res = keep.tile([P, n], F32, name=f"res{c}_{m}")
-                if last and m % 2 == 1:
-                    nc.vector.tensor_copy(res[:], accs[m][:])
+            for b, acc in enumerate(accs):
+                res = keep.tile([P, share, n], F32, name=f"res{c}_{b}")
+                if last and b == 1:
+                    nc.vector.tensor_copy(res[:], acc[:])
                 else:
-                    nc.scalar.copy(res[:], accs[m][:])
-                queue = nc.scalar if last and m % 2 == 0 else nc.sync
-                queue.dma_start(out[m * P : (m + 1) * P, v0 : v0 + n], res[:])
+                    nc.scalar.copy(res[:], acc[:])
+                queue = nc.scalar if last and b == 0 else nc.sync
+                queue.dma_start(out_rows[:, b * share : (b + 1) * share, v0 : v0 + n], res[:])
 
-        for c, (v0, n) in enumerate(CHUNKS):
-            h, part = v0 // HALF, slice(v0 % HALF, v0 % HALF + n)
-            z_bf = combine(lo_a[:, :, v0 : v0 + n], lo_b[h][:, :, part], ALU.add, n, f"z_bf{c}")
-            if c > 0:
-                finish(c - 1, accs, z2_bf)
-            accs = [
-                psum.tile([P, n], F32, name=f"out_acc{c}_{m}", tag=f"bank{(4 * c + m) % 8}") for m in range(N // P)
-            ]
-            product(accs, w2_q, quantize(z_bf, n, f"z{c}"), True)
-            if h == 0:
-                grouped = keep.tile([P, n, PACK], BF16, name=f"z2_bf{c}", align_bytes=64)
-                nc.vector.tensor_tensor(
-                    grouped[:].rearrange("p v (u e) -> p v u e", e=2),
-                    hi_a[h][:].rearrange("p u v e -> p v u e"),
-                    hi_b[h][:].rearrange("p u v e -> p v u e"),
-                    ALU.subtract,
-                )
-                z2_bf = grouped[:].rearrange("p w j -> p (w j)")
-            else:
-                z2_bf = combine(hi_a[h][:, :, part], hi_b[h][:, :, part], ALU.subtract, n, f"z2_bf{c}")
-        finish(len(CHUNKS) - 1, accs, z2_bf)
+        z_bf0 = join_low(0)
+        fetch_left(1, 0)
+        for t in range(PACK):
+            if t + 1 < PACK:
+                fetch_left(1, t + 1)
+            shrink_terms(0, t, slice(0, HALF))
+            fetch_right(1, t)
+            if t == 0:
+                accs0 = open_sums(0)
+                product(accs0, w2_q, quantize(z_bf0, HALF, "z0"), True)
+        z2_bf0 = join_high(0)
+        for t in range(PACK - 1):
+            shrink_terms(1, t, slice(0, HALF))
+        for part in (slice(0, P), slice(P, HALF)):
+            shrink_terms(1, PACK - 1, part)
+        z_bf1 = join_low(1)
+        product(accs0, w3_q, quantize(z2_bf0, HALF, "z20"), False)
+        store(0, accs0)
+        z_q1 = quantize(z_bf1, HALF, "z1")
+        accs1, accs2 = open_sums(1), open_sums(2)
+        product(accs1, w2_q, z_q1, True, slice(0, P))
+        product(accs2, w2_q, z_q1, True, slice(P, HALF))
+        z2_bf1 = join_high(1)
+        z2_bf2 = join_high(2)
+        product(accs1, w3_q, quantize(z2_bf1, P, "z21"), False)
+        store(1, accs1)
+        product(accs2, w3_q, quantize(z2_bf2, P, "z22"), False)
+        store(2, accs2)

@@ -220,15 +220,21 @@ def tile_picked_haarthr_none_p_kernel(
             fetch_right(0, t)
 
         def join_low(h):
+            pairs = keep.tile([P, 2, HALF, 2], BF16, name=f"z_pairs{h}", align_bytes=64)
+            for u in range(2):
+                nc.vector.scalar_tensor_tensor(
+                    pairs[:, u],
+                    lf[h][:, 2 * u : 2 * u + 2, :].rearrange("p e c -> p c e"),
+                    2.0,
+                    dn[h][:, 2 * u : 2 * u + 2, :].rearrange("p e c -> p c e"),
+                    ALU.mult,
+                    ALU.add,
+                )
+            return pairs
+
+        def weave(pairs, h):
             grouped = keep.tile([P, HALF, PACK], BF16, name=f"z_bf{h}", align_bytes=64)
-            nc.vector.scalar_tensor_tensor(
-                grouped[:],
-                lf[h][:].rearrange("p t c -> p c t"),
-                2.0,
-                dn[h].rearrange("p t c -> p c t"),
-                ALU.mult,
-                ALU.add,
-            )
+            nc.vector.tensor_copy(grouped[:].bitcast(F32), pairs[:].bitcast(F32).rearrange("p u c o -> p c (u o)"))
             return grouped[:].rearrange("p w j -> p (w j)")
 
         def join_high(c):
@@ -278,7 +284,7 @@ def tile_picked_haarthr_none_p_kernel(
                 queue = nc.scalar if last and b == 0 else nc.sync
                 queue.dma_start(out_rows[:, b * share : (b + 1) * share, v0 : v0 + n], res[:])
 
-        z_bf0 = join_low(0)
+        z_pairs0 = join_low(0)
         fetch_left(1, 0)
         for t in range(PACK):
             if t + 1 < PACK:
@@ -286,6 +292,8 @@ def tile_picked_haarthr_none_p_kernel(
             shrink_terms(0, t, slice(0, HALF))
             fetch_right(1, t)
             if t == 0:
+                z_bf0 = weave(z_pairs0, 0)
+            if t == 1:
                 accs0 = open_sums(0)
                 product(accs0, w2_q, quantize(z_bf0, HALF, "z0"), True)
         z2_bf0 = join_high(0)
@@ -293,16 +301,17 @@ def tile_picked_haarthr_none_p_kernel(
             shrink_terms(1, t, slice(0, HALF))
         for part in (slice(0, P), slice(P, HALF)):
             shrink_terms(1, PACK - 1, part)
-        z_bf1 = join_low(1)
+        z_pairs1 = join_low(1)
         product(accs0, w3_q, quantize(z2_bf0, HALF, "z20"), False)
         store(0, accs0)
+        z_bf1 = weave(z_pairs1, 1)
+        z2_bf1 = join_high(1)
         z_q1 = quantize(z_bf1, HALF, "z1")
         accs1, accs2 = open_sums(1), open_sums(2)
         product(accs1, w2_q, z_q1, True, slice(0, P))
-        product(accs2, w2_q, z_q1, True, slice(P, HALF))
-        z2_bf1 = join_high(1)
         z2_bf2 = join_high(2)
         product(accs1, w3_q, quantize(z2_bf1, P, "z21"), False)
         store(1, accs1)
+        product(accs2, w2_q, z_q1, True, slice(P, HALF))
         product(accs2, w3_q, quantize(z2_bf2, P, "z22"), False)
         store(2, accs2)

@@ -23,6 +23,7 @@ HALF_BYTES = PACK * HALF * 4
 X_HEAD = 640
 S_HEAD = 768
 W1_HEAD = 256
+W2_SCALAR = 128
 TINY = 2.0**-80
 CHUNKS = ((0, 256), (256, 128), (384, 128))
 
@@ -50,7 +51,10 @@ def tile_picked_haarthr_none_p_kernel(
             keep.tile([P, PACK, cols.stop - cols.start], F32, name=f"w1_raw{part}") for part, cols in enumerate(w1_cols)
         ]
         w1_rows = w1.rearrange("(p j) c -> p j c", j=PACK)
-        w2_raw = [keep.tile([P, PACK, N // 2], F32, name=f"w2_raw{half}", tag=f"w2_then_y{half}") for half in range(2)]
+        w2_raw = [
+            keep.tile([P, PACK, W2_SCALAR], F32, name="w2_raw0", tag="w2_then_y0", align_bytes=64),
+            keep.tile([P, PACK, N - W2_SCALAR], F32, name="w2_raw1"),
+        ]
         w2_rows = w2.rearrange("(p j) c -> p j c", j=PACK)
         w3_then_dn = keep.tile([P, PACK * N], F32, name="w3_then_dn")
         w3_raw = w3_then_dn[:].rearrange("p (j c) -> p j c", j=PACK)
@@ -67,10 +71,10 @@ def tile_picked_haarthr_none_p_kernel(
         for part, cols in enumerate(w1_cols):
             nc.sync.dma_start(w1_raw[part][:], w1_rows[:, :, cols])
         nc.sync.dma_start(gh_sb[:], gh.rearrange("(p t) o -> p (t o)", t=PACK))
-        nc.sync.dma_start(w2_raw[0][:], w2_rows[:, :, : N // 2])
+        nc.sync.dma_start(w2_raw[0][:], w2_rows[:, :, :W2_SCALAR])
         nc.sync.dma_start(left_sb[:], left)
         nc.sync.dma_start(right_sb[:], right)
-        nc.sync.dma_start(w2_raw[1][:], w2_rows[:, :, N // 2 :])
+        nc.sync.dma_start(w2_raw[1][:], w2_rows[:, :, W2_SCALAR:])
         nc.sync.dma_start(w3_raw, w3.rearrange("(p j) c -> p j c", j=PACK))
 
         xq_scale = keep.tile([P, S], U8, name="xq_scale", align_bytes=64)
@@ -80,12 +84,10 @@ def tile_picked_haarthr_none_p_kernel(
 
         gl_abs = keep.tile([P, PACK], F32, name="gl_abs")
         gl_lift = keep.tile([P, PACK], F32, name="gl_lift")
-        gain = reuse.tile([P, PACK], F32, name="gain", offset=0)
-        gain_last = reuse.tile([P, 1], F32, name="gain_last", offset=2 * HALF_BYTES)
+        gain = reuse.tile([P, 16], F32, name="gain", offset=2 * HALF_BYTES - 32)[:, :PACK]
         nc.scalar.activation(gl_abs[:], gl_sb[:], ACT.Abs)
         nc.gpsimd.tensor_scalar(gl_lift[:], gl_abs[:], TINY, 2.0 * TINY, ALU.is_lt, ALU.mult)
-        nc.gpsimd.tensor_tensor(gain[:], gl_sb[:], gl_lift[:], ALU.add)
-        nc.gpsimd.tensor_tensor(gain_last[:], gl_sb[:, PACK - 1 :], gl_lift[:, PACK - 1 :], ALU.add)
+        nc.gpsimd.tensor_tensor(gain, gl_sb[:], gl_lift[:], ALU.add)
 
         w1_bf = [
             keep.tile([P, 2, P, PACK], BF16, name=f"w1_bf{pair}", tag=f"w1_bf{pair}", align_bytes=64)
@@ -114,24 +116,22 @@ def tile_picked_haarthr_none_p_kernel(
         slope, slope_neg, knee, knee_neg = (
             keep.tile([P, PACK], F32, name=name) for name in ("slope", "slope_neg", "knee", "knee_neg")
         )
-        nc.vector.reciprocal(gain_inv[:], gain[:])
+        nc.vector.reciprocal(gain_inv[:], gain)
         nc.vector.scalar_tensor_tensor(slope[:], gain_inv[:], 0.75, gh_sb[:], ALU.mult, ALU.mult)
         nc.scalar.activation(knee[:], gh_sb[:], ACT.Abs, scale=0.5)
         nc.scalar.activation(knee_neg[:], knee[:], ACT.Copy, scale=-1.0)
         nc.scalar.activation(slope_neg[:], slope[:], ACT.Copy, scale=-1.0)
 
-        def quantize(grouped, width, name):
-            word = keep.tile([P, width], U32, name=f"{name}_word", align_bytes=64)
+        def quantize(grouped, width, name, tag=None):
+            word = keep.tile([P, width], U32, name=f"{name}_word", tag=tag or f"{name}_word", align_bytes=64)
             scale = keep.tile([P, width], U8, name=f"{name}_scale", align_bytes=64)
             nc.vector.quantize_mx(out=word[:].bitcast(FP8X4), scales=scale[:], in_=grouped)
             return word, scale
 
-        def cast(dst, raw):
-            nc.vector.tensor_copy(
-                dst.rearrange("p (c i) j -> p c j i", i=4), raw.rearrange("p j (c i) -> p c j i", i=4)
-            )
+        def cast(dst, raw, copy=nc.vector.tensor_copy):
+            copy(dst.rearrange("p (c i) j -> p c j i", i=4), raw.rearrange("p j (c i) -> p c j i", i=4))
 
-        y = [keep.tile([P, S], F32, name=f"y{t}", tag="w2_then_y0" if t == 1 else f"y{t}") for t in range(PACK)]
+        y = [keep.tile([P, S], F32, name=f"y{t}", tag="w2_then_y0" if t == 0 else f"y{t}", align_bytes=64) for t in range(PACK)]
         lf = [
             keep.tile([P, PACK, HALF], F32, name="lf0"),
             reuse.tile([P, PACK, HALF], F32, name="lf1", offset=2 * HALF_BYTES),
@@ -148,9 +148,8 @@ def tile_picked_haarthr_none_p_kernel(
         hi_b = [hi[h][:, 1] for h in range(2)]
 
         y_acc = {}
-        pieces = [(0, 0, BANK), (0, BANK, S_HEAD), (0, S_HEAD, S)]
-        pieces = pieces + [(t, s0, s0 + BANK) for s0 in (0, BANK) for t in (1, 2)]
-        pieces = pieces + [(3, s0, s0 + BANK) for s0 in (0, BANK)]
+        pieces = [(0, 0, BANK), (1, 0, BANK), (0, BANK, S_HEAD), (0, S_HEAD, S), (1, BANK, S)]
+        pieces = pieces + [(t, s0, s0 + BANK) for t in (2, 3) for s0 in (0, BANK)]
         for step, (t, s0, s1) in enumerate(pieces):
             cols = slice(t * P, (t + 1) * P)
             acc = psum.tile([P, s1 - s0], F32, name=f"y_acc{t}_{s0}", tag=f"bank{step % 8}")
@@ -171,11 +170,10 @@ def tile_picked_haarthr_none_p_kernel(
         def copy_y(t, s0):
             acc = y_acc[t, s0]
             window = y[t][:, s0 : s0 + acc.shape[1]]
-            if t == 1:
+            if (t, s0) == (1, 0):
                 nc.vector.tensor_scalar(window, acc[:], gain[:, t : t + 1], None, ALU.mult)
             else:
-                factor = gain_last[:] if (t, s0) == (PACK - 1, BANK) else gain[:, t : t + 1]
-                nc.scalar.activation(window, acc[:], ACT.Copy, scale=factor)
+                nc.scalar.activation(window, acc[:], ACT.Copy, scale=gain[:, t : t + 1])
 
         def fetch_left(h, t):
             nc.scalar.activation(lf[h][:, t, :], y[t][:].indirect(left_sb[:, h * 16 : (h + 1) * 16]), ACT.Copy)
@@ -194,47 +192,58 @@ def tile_picked_haarthr_none_p_kernel(
                 hi_b[h][:, t, part], dn[h][:, t, part], ACT.Relu, scale=slope[:, one], bias=knee_neg[:, one]
             )
 
-        w23_bf = keep.tile([P, 2 * N, PACK], BF16, name="w23_bf", align_bytes=64)
-        w2_bf, w3_bf = w23_bf[:, :N, :], w23_bf[:, N:, :]
-        cast(w2_bf[:, : N // 2, :], w2_raw[0][:])
+        w2_bf = keep.tile([P, N, PACK], BF16, name="w2_bf", align_bytes=64)
+        w3_bf = keep.tile([P, N, PACK], BF16, name="w3_bf", align_bytes=64)
+        w2_q = (
+            keep.tile([P, N], U32, name="w2_word", align_bytes=64),
+            keep.tile([P, N], U8, name="w2_scale", align_bytes=64),
+        )
+        cast(w2_bf[:, :W2_SCALAR, :], w2_raw[0][:], nc.scalar.copy)
         for s0 in (0, BANK, S_HEAD):
             copy_y(0, s0)
         copy_y(1, 0)
+        cast(w2_bf[:, W2_SCALAR : N // 2, :], w2_raw[1][:, :, : N // 2 - W2_SCALAR])
+        cast(w2_bf[:, N // 2 :, :], w2_raw[1][:, :, N // 2 - W2_SCALAR :])
+        for half in range(2):
+            cols = slice(half * (N // 2), (half + 1) * (N // 2))
+            nc.vector.quantize_mx(
+                out=w2_q[0][:, cols].bitcast(FP8X4),
+                scales=w2_q[1][:, cols],
+                in_=w2_bf[:, cols, :].rearrange("p w j -> p (w j)"),
+            )
         copy_y(1, BANK)
-        cast(w2_bf[:, N // 2 :, :], w2_raw[1][:])
-        copy_y(2, 0)
         fetch_left(0, 0)
-        copy_y(2, BANK)
         for half in range(2):
             cols = slice(half * (N // 2), (half + 1) * (N // 2))
             cast(w3_bf[:, cols, :], w3_raw[:, :, cols])
         fetch_right(0, 0)
-        w23_word, w23_scale = quantize(w23_bf[:].rearrange("p w j -> p (w j)"), 2 * N, "w23")
-        w2_q, w3_q = (w23_word[:, :N], w23_scale[:, :N]), (w23_word[:, N:], w23_scale[:, N:])
-        copy_y(3, 0)
+        w3_q = quantize(w3_bf[:].rearrange("p w j -> p (w j)"), N, "w3")
+        copy_y(2, 0)
         fetch_left(0, 1)
         fetch_right(0, 1)
+        copy_y(2, BANK)
+        copy_y(3, 0)
         copy_y(3, BANK)
         for t in (2, 3):
             fetch_left(0, t)
             fetch_right(0, t)
 
-        def join_low(h):
-            pairs = keep.tile([P, 2, HALF, 2], BF16, name=f"z_pairs{h}", align_bytes=64)
-            for u in range(2):
-                nc.vector.scalar_tensor_tensor(
-                    pairs[:, u],
-                    lf[h][:, 2 * u : 2 * u + 2, :].rearrange("p e c -> p c e"),
-                    2.0,
-                    dn[h][:, 2 * u : 2 * u + 2, :].rearrange("p e c -> p c e"),
-                    ALU.mult,
-                    ALU.add,
-                )
-            return pairs
+        z_pairs = [keep.tile([P, 2, HALF, 2], BF16, name=f"z_pairs{h}", align_bytes=64) for h in range(2)]
 
-        def weave(pairs, h):
+        def join_low(h, u):
+            nc.vector.scalar_tensor_tensor(
+                z_pairs[h][:, u],
+                lf[h][:, 2 * u : 2 * u + 2, :].rearrange("p e c -> p c e"),
+                2.0,
+                dn[h][:, 2 * u : 2 * u + 2, :].rearrange("p e c -> p c e"),
+                ALU.mult,
+                ALU.add,
+            )
+
+        def weave(h):
             grouped = keep.tile([P, HALF, PACK], BF16, name=f"z_bf{h}", align_bytes=64)
-            nc.vector.tensor_copy(grouped[:].bitcast(F32), pairs[:].bitcast(F32).rearrange("p u c o -> p c (u o)"))
+            copy = nc.scalar.copy if h == 1 else nc.vector.tensor_copy
+            copy(grouped[:].bitcast(F32), z_pairs[h][:].bitcast(F32).rearrange("p u c o -> p c (u o)"))
             return grouped[:].rearrange("p w j -> p (w j)")
 
         def join_high(c):
@@ -250,7 +259,7 @@ def tile_picked_haarthr_none_p_kernel(
             return grouped[:].rearrange("p w j -> p (w j)")
 
         out_rows = out.rearrange("(m p) v -> p m v", p=P)
-        BANKS = ((0, 1), (2,), (3, 4))
+        BANKS = ((0, 1), (2, 7), (3, 4, 5, 6))
 
         def open_sums(c):
             n = CHUNKS[c][1]
@@ -277,14 +286,15 @@ def tile_picked_haarthr_none_p_kernel(
             last = c == len(CHUNKS) - 1
             for b, acc in enumerate(accs):
                 res = keep.tile([P, share, n], F32, name=f"res{c}_{b}")
-                if last and b == 1:
+                if (c, b) in ((1, 0), (2, 1), (2, 3)):
                     nc.vector.tensor_copy(res[:], acc[:])
                 else:
                     nc.scalar.copy(res[:], acc[:])
-                queue = nc.scalar if last and b == 0 else nc.sync
+                queue = nc.scalar if last and b % 2 == 0 else nc.sync
                 queue.dma_start(out_rows[:, b * share : (b + 1) * share, v0 : v0 + n], res[:])
 
-        z_pairs0 = join_low(0)
+        for u in range(2):
+            join_low(0, u)
         fetch_left(1, 0)
         for t in range(PACK):
             if t + 1 < PACK:
@@ -292,26 +302,27 @@ def tile_picked_haarthr_none_p_kernel(
             shrink_terms(0, t, slice(0, HALF))
             fetch_right(1, t)
             if t == 0:
-                z_bf0 = weave(z_pairs0, 0)
-            if t == 1:
-                accs0 = open_sums(0)
-                product(accs0, w2_q, quantize(z_bf0, HALF, "z0"), True)
+                z_bf0 = weave(0)
+            if t == 2:
+                join_low(1, 0)
+        accs0 = open_sums(0)
+        product(accs0, w2_q, quantize(z_bf0, HALF, "z0", "y2"), True)
         z2_bf0 = join_high(0)
         for t in range(PACK - 1):
             shrink_terms(1, t, slice(0, HALF))
         for part in (slice(0, P), slice(P, HALF)):
             shrink_terms(1, PACK - 1, part)
-        z_pairs1 = join_low(1)
+        join_low(1, 1)
+        z_bf1 = weave(1)
         product(accs0, w3_q, quantize(z2_bf0, HALF, "z20"), False)
         store(0, accs0)
-        z_bf1 = weave(z_pairs1, 1)
         z2_bf1 = join_high(1)
         z_q1 = quantize(z_bf1, HALF, "z1")
         accs1, accs2 = open_sums(1), open_sums(2)
         product(accs1, w2_q, z_q1, True, slice(0, P))
+        product(accs2, w2_q, z_q1, True, slice(P, HALF))
         z2_bf2 = join_high(2)
         product(accs1, w3_q, quantize(z2_bf1, P, "z21"), False)
         store(1, accs1)
-        product(accs2, w2_q, z_q1, True, slice(P, HALF))
         product(accs2, w3_q, quantize(z2_bf2, P, "z22"), False)
         store(2, accs2)

@@ -63,10 +63,8 @@ def tile_picked_haarthr_none_p_kernel(
         nc.vector.memset(x_scale_sb[:].bitcast(I32), 0)
         nc.sync.dma_start(x_word_sb[:, :X_HEAD].bitcast(I32), x_rows[:, :X_HEAD])
         nc.sync.dma_start(gl_sb[:], gl.rearrange("(p t) o -> p (t o)", t=PACK))
-        for q in range(4):
-            nc.sync.dma_start(
-                x_scale_sb[32 * q : 32 * q + 4, :].bitcast(I32), x_scales[0, 4 * q : 4 * q + 4, :].bitcast(I32)
-            )
+        for r in range(4):
+            nc.sync.dma_start(x_scale_sb[r:P:32, :].bitcast(I32), x_scales[0, r:16:4, :].bitcast(I32))
         nc.sync.dma_start(x_word_sb[:, X_HEAD:].bitcast(I32), x_rows[:, X_HEAD:])
         for part, cols in enumerate(w1_cols):
             nc.sync.dma_start(w1_raw[part][:], w1_rows[:, :, cols])

from contextlib import ExitStack

import concourse.mybir as mybir

K, T, S, V, N, H = 512, 2048, 1024, 512, 512, 512
FLOPS = 2 * K * H * S + 2 * 2 * H * N * V

F32 = mybir.dt.float32
BF16 = mybir.dt.bfloat16
I32 = mybir.dt.int32
U32 = mybir.dt.uint32
U16 = mybir.dt.uint16
U8 = mybir.dt.uint8
FP8X4 = mybir.dt.float8_e4m3fn_x4
ALU = mybir.AluOpType
ACT = mybir.ActivationFunctionType

P = 128
PACK = 4
BANK = 512
HALF = V // 2
HALF_BYTES = PACK * HALF * 4
X_HEAD = 640
S_HEAD = 768
W1_HEAD = 256
W2_SCALAR = 128
TINY = 2.0**-80
CHUNKS = ((0, 256), (256, 128), (384, 128))


def tile_picked_haarthr_none_p_kernel(
    tc, x_words, x_scales, w1, gl, gh, w2, w3, offs, left, right, out
):
    nc = tc.nc
    with ExitStack() as ctx:
        keep = ctx.enter_context(tc.tile_pool(name="keep", bufs=1))
        reuse = ctx.enter_context(tc.tile_pool(name="reuse", bufs=1))
        psum = ctx.enter_context(tc.psum_pool(name="psum", bufs=1))

        offs_sb = keep.tile([P, S // 16], U16, name="offs_sb")
        left_sb = keep.tile([P, V // 16], U16, name="left_sb")
        right_sb = keep.tile([P, V // 16], U16, name="right_sb")
        nc.sync.dma_start(offs_sb[:], offs)

        x_scale_sb = keep.tile([P, T], U8, name="x_scale_sb", align_bytes=64)
        x_word_sb = keep.tile([P, T], U32, name="x_word_sb", align_bytes=64)
        gl_sb = keep.tile([P, PACK], F32, name="gl_sb")
        gh_sb = keep.tile([P, PACK], F32, name="gh_sb")
        w1_cols = (slice(0, W1_HEAD), slice(W1_HEAD, H))
        w1_raw = [
            keep.tile([P, PACK, cols.stop - cols.start], F32, name=f"w1_raw{part}") for part, cols in enumerate(w1_cols)
        ]
        w1_rows = w1.rearrange("(p j) c -> p j c", j=PACK)
        w2_raw = [
            keep.tile([P, PACK, W2_SCALAR], F32, name="w2_raw0", tag="w2_then_y0", align_bytes=64),
            keep.tile([P, PACK, N - W2_SCALAR], F32, name="w2_raw1"),
        ]
        w2_rows = w2.rearrange("(p j) c -> p j c", j=PACK)
        w3_then_dn = keep.tile([P, PACK * N], F32, name="w3_then_dn")
        w3_raw = w3_then_dn[:].rearrange("p (j c) -> p j c", j=PACK)
        x_rows = x_words[0].rearrange("p c r -> p (c r)").bitcast(I32)

        nc.vector.memset(x_scale_sb[:].bitcast(I32), 0)
        nc.sync.dma_start(x_word_sb[:, :X_HEAD].bitcast(I32), x_rows[:, :X_HEAD])
        nc.sync.dma_start(gl_sb[:], gl.rearrange("(p t) o -> p (t o)", t=PACK))
        for r in range(4):
            nc.sync.dma_start(x_scale_sb[r:P:32, :].bitcast(I32), x_scales[0, r:16:4, :].bitcast(I32))
        nc.sync.dma_start(x_word_sb[:, X_HEAD:].bitcast(I32), x_rows[:, X_HEAD:])
        for part, cols in enumerate(w1_cols):
            nc.sync.dma_start(w1_raw[part][:], w1_rows[:, :, cols])
        nc.sync.dma_start(gh_sb[:], gh.rearrange("(p t) o -> p (t o)", t=PACK))
        nc.sync.dma_start(w2_raw[0][:], w2_rows[:, :, :W2_SCALAR])
        nc.sync.dma_start(left_sb[:], left)
        nc.sync.dma_start(right_sb[:], right)
        nc.sync.dma_start(w2_raw[1][:], w2_rows[:, :, W2_SCALAR:])
        nc.sync.dma_start(w3_raw, w3.rearrange("(p j) c -> p j c", j=PACK))

        xq_scale = keep.tile([P, S], U8, name="xq_scale", align_bytes=64)
        xq_head = keep.tile([P, S_HEAD], U32, name="xq_head", align_bytes=64)
        nc.vector.tensor_copy(xq_scale[:], x_scale_sb[:].indirect(offs_sb[:]))
        nc.vector.tensor_copy(xq_head[:], x_word_sb[:].indirect(offs_sb[:, : S_HEAD // 16]))

        gl_abs = keep.tile([P, PACK], F32, name="gl_abs")
        gl_lift = keep.tile([P, PACK], F32, name="gl_lift")
        gain = reuse.tile([P, 16], F32, name="gain", offset=2 * HALF_BYTES - 32)[:, :PACK]
        nc.scalar.activation(gl_abs[:], gl_sb[:], ACT.Abs)
        nc.gpsimd.tensor_scalar(gl_lift[:], gl_abs[:], TINY, 2.0 * TINY, ALU.is_lt, ALU.mult)
        nc.gpsimd.tensor_tensor(gain, gl_sb[:], gl_lift[:], ALU.add)

        w1_bf = [
            keep.tile([P, 2, P, PACK], BF16, name=f"w1_bf{pair}", tag=f"w1_bf{pair}", align_bytes=64)
            for pair in range(2)
        ]
        for part, cols in enumerate(w1_cols):
            for pair in range(2):
                nc.scalar.copy(
                    w1_bf[pair][:, :, cols.start // PACK : cols.stop // PACK, :].rearrange("p t m j -> p m j t"),
                    w1_raw[part][:].rearrange("p j (m t) -> p m j t", t=PACK)[:, :, :, 2 * pair : 2 * pair + 2],
                )

        w1_word = keep.tile([P, H], U32, name="w1_word", align_bytes=64)
        w1_scale = keep.tile([P, H], U8, name="w1_scale", align_bytes=64)
        xq_tail = keep.tile([P, S - S_HEAD], U32, name="xq_tail", tag="w1_bf0", align_bytes=64)
        for pair in range(2):
            cols = slice(2 * pair * P, (2 * pair + 2) * P)
            nc.vector.quantize_mx(
                out=w1_word[:, cols].bitcast(FP8X4),
                scales=w1_scale[:, cols],
                in_=w1_bf[pair][:].rearrange("p t m j -> p (t m j)"),
            )
            if pair == 0:
                nc.vector.tensor_copy(xq_tail[:], x_word_sb[:].indirect(offs_sb[:, S_HEAD // 16 :]))
        gain_inv = keep.tile([P, PACK], F32, name="gain_inv")
        slope, slope_neg, knee, knee_neg = (
            keep.tile([P, PACK], F32, name=name) for name in ("slope", "slope_neg", "knee", "knee_neg")
        )
        nc.vector.reciprocal(gain_inv[:], gain)
        nc.vector.scalar_tensor_tensor(slope[:], gain_inv[:], 0.75, gh_sb[:], ALU.mult, ALU.mult)
        nc.scalar.activation(knee[:], gh_sb[:], ACT.Abs, scale=0.5)
        nc.scalar.activation(knee_neg[:], knee[:], ACT.Copy, scale=-1.0)
        nc.scalar.activation(slope_neg[:], slope[:], ACT.Copy, scale=-1.0)

        def quantize(grouped, width, name, tag=None):
            word = keep.tile([P, width], U32, name=f"{name}_word", tag=tag or f"{name}_word", align_bytes=64)
            scale = keep.tile([P, width], U8, name=f"{name}_scale", align_bytes=64)
            nc.vector.quantize_mx(out=word[:].bitcast(FP8X4), scales=scale[:], in_=grouped)
            return word, scale

        def cast(dst, raw, copy=nc.vector.tensor_copy):
            copy(dst.rearrange("p (c i) j -> p c j i", i=4), raw.rearrange("p j (c i) -> p c j i", i=4))

        y = [keep.tile([P, S], F32, name=f"y{t}", tag="w2_then_y0" if t == 0 else f"y{t}", align_bytes=64) for t in range(PACK)]
        lf = [
            keep.tile([P, PACK, HALF], F32, name="lf0"),
            reuse.tile([P, PACK, HALF], F32, name="lf1", offset=2 * HALF_BYTES),
        ]
        dn = [
            w3_raw[:, :, :HALF],
            w3_raw[:, :, HALF:],
        ]
        hi = [
            reuse.tile([P, 2, PACK, HALF], F32, name="hi0", offset=0),
            keep.tile([P, 2, PACK, HALF], F32, name="hi1"),
        ]
        hi_a = [hi[h][:, 0] for h in range(2)]
        hi_b = [hi[h][:, 1] for h in range(2)]

        y_acc = {}
        pieces = [(0, 0, BANK), (1, 0, BANK), (0, BANK, S_HEAD), (0, S_HEAD, S), (1, BANK, S)]
        pieces = pieces + [(t, s0, s0 + BANK) for t in (2, 3) for s0 in (0, BANK)]
        for step, (t, s0, s1) in enumerate(pieces):
            cols = slice(t * P, (t + 1) * P)
            acc = psum.tile([P, s1 - s0], F32, name=f"y_acc{t}_{s0}", tag=f"bank{step % 8}")
            y_acc[t, s0] = acc
            parts = (s0, S_HEAD, s1) if s0 < S_HEAD < s1 else (s0, s1)
            for a, b in zip(parts[:-1], parts[1:]):
                words = xq_head[:, a:b] if b <= S_HEAD else xq_tail[:, a - S_HEAD : b - S_HEAD]
                nc.tensor.matmul_mx(
                    out=acc[:, a - s0 : b - s0],
                    lhsT=w1_word[:, cols].bitcast(FP8X4),
                    lhsT_scale=w1_scale[:, cols],
                    rhs=words.bitcast(FP8X4),
                    rhs_scale=xq_scale[:, a:b],
                    start=True,
                    stop=True,
                )

        def copy_y(t, s0):
            acc = y_acc[t, s0]
            window = y[t][:, s0 : s0 + acc.shape[1]]
            if (t, s0) == (1, 0):
                nc.vector.tensor_scalar(window, acc[:], gain[:, t : t + 1], None, ALU.mult)
            else:
                nc.scalar.activation(window, acc[:], ACT.Copy, scale=gain[:, t : t + 1])

        def fetch_left(h, t):
            nc.scalar.activation(lf[h][:, t, :], y[t][:].indirect(left_sb[:, h * 16 : (h + 1) * 16]), ACT.Copy)

        def fetch_right(h, t):
            nc.vector.tensor_tensor(
                dn[h][:, t, :], y[t][:].indirect(right_sb[:, h * 16 : (h + 1) * 16]), lf[h][:, t, :], ALU.subtract
            )

        def shrink_terms(h, t, part):
            one = slice(t, t + 1)
            nc.scalar.activation(
                hi_a[h][:, t, part], dn[h][:, t, part], ACT.Relu, scale=slope_neg[:, one], bias=knee_neg[:, one]
            )
            nc.scalar.activation(
                hi_b[h][:, t, part], dn[h][:, t, part], ACT.Relu, scale=slope[:, one], bias=knee_neg[:, one]
            )

        w2_bf = keep.tile([P, N, PACK], BF16, name="w2_bf", align_bytes=64)
        w3_bf = keep.tile([P, N, PACK], BF16, name="w3_bf", align_bytes=64)
        w2_q = (
            keep.tile([P, N], U32, name="w2_word", align_bytes=64),
            keep.tile([P, N], U8, name="w2_scale", align_bytes=64),
        )
        cast(w2_bf[:, :W2_SCALAR, :], w2_raw[0][:], nc.scalar.copy)
        for s0 in (0, BANK, S_HEAD):
            copy_y(0, s0)
        copy_y(1, 0)
        cast(w2_bf[:, W2_SCALAR : N // 2, :], w2_raw[1][:, :, : N // 2 - W2_SCALAR])
        cast(w2_bf[:, N // 2 :, :], w2_raw[1][:, :, N // 2 - W2_SCALAR :])
        for half in range(2):
            cols = slice(half * (N // 2), (half + 1) * (N // 2))
            nc.vector.quantize_mx(
                out=w2_q[0][:, cols].bitcast(FP8X4),
                scales=w2_q[1][:, cols],
                in_=w2_bf[:, cols, :].rearrange("p w j -> p (w j)"),
            )
        copy_y(1, BANK)
        fetch_left(0, 0)
        for half in range(2):
            cols = slice(half * (N // 2), (half + 1) * (N // 2))
            cast(w3_bf[:, cols, :], w3_raw[:, :, cols])
        fetch_right(0, 0)
        w3_q = quantize(w3_bf[:].rearrange("p w j -> p (w j)"), N, "w3")
        copy_y(2, 0)
        fetch_left(0, 1)
        fetch_right(0, 1)
        copy_y(2, BANK)
        copy_y(3, 0)
        copy_y(3, BANK)
        for t in (2, 3):
            fetch_left(0, t)
            fetch_right(0, t)

        z_pairs = [keep.tile([P, 2, HALF, 2], BF16, name=f"z_pairs{h}", align_bytes=64) for h in range(2)]

        def join_low(h, u):
            nc.vector.scalar_tensor_tensor(
                z_pairs[h][:, u],
                lf[h][:, 2 * u : 2 * u + 2, :].rearrange("p e c -> p c e"),
                2.0,
                dn[h][:, 2 * u : 2 * u + 2, :].rearrange("p e c -> p c e"),
                ALU.mult,
                ALU.add,
            )

        def weave(h):
            grouped = keep.tile([P, HALF, PACK], BF16, name=f"z_bf{h}", align_bytes=64)
            copy = nc.scalar.copy if h == 1 else nc.vector.tensor_copy
            copy(grouped[:].bitcast(F32), z_pairs[h][:].bitcast(F32).rearrange("p u c o -> p c (u o)"))
            return grouped[:].rearrange("p w j -> p (w j)")

        def join_high(c):
            v0, n = CHUNKS[c]
            h, part = v0 // HALF, slice(v0 % HALF, v0 % HALF + n)
            grouped = keep.tile([P, n, PACK], BF16, name=f"z2_bf{c}", align_bytes=64)
            nc.vector.tensor_tensor(
                grouped[:].rearrange("p (c i) t -> p c t i", i=4),
                hi_a[h][:, :, part].rearrange("p t (c i) -> p c t i", i=4),
                hi_b[h][:, :, part].rearrange("p t (c i) -> p c t i", i=4),
                ALU.subtract,
            )
            return grouped[:].rearrange("p w j -> p (w j)")

        out_rows = out.rearrange("(m p) v -> p m v", p=P)
        BANKS = ((0, 1), (2, 7), (3, 4, 5, 6))

        def open_sums(c):
            n = CHUNKS[c][1]
            share = (N // P) // len(BANKS[c])
            return [psum.tile([P, share, n], F32, name=f"out_acc{c}_{b}", tag=f"bank{b}") for b in BANKS[c]]

        def product(accs, w_q, act_q, first, part=slice(None)):
            share = (N // P) // len(accs)
            for m in range(N // P):
                cols = slice(m * P, (m + 1) * P)
                nc.tensor.matmul_mx(
                    out=accs[m // share][:, m % share, :],
                    lhsT=w_q[0][:, cols].bitcast(FP8X4),
                    lhsT_scale=w_q[1][:, cols],
                    rhs=act_q[0][:, part].bitcast(FP8X4),
                    rhs_scale=act_q[1][:, part],
                    start=first and m % share == 0,
                    stop=not first and m % share == share - 1,
                )

        def store(c, accs):
            v0, n = CHUNKS[c]
            share = (N // P) // len(accs)
            last = c == len(CHUNKS) - 1
            for b, acc in enumerate(accs):
                res = keep.tile([P, share, n], F32, name=f"res{c}_{b}")
                if (c, b) in ((1, 0), (2, 1), (2, 3)):
                    nc.vector.tensor_copy(res[:], acc[:])
                else:
                    nc.scalar.copy(res[:], acc[:])
                queue = nc.scalar if last and b % 2 == 0 else nc.sync
                queue.dma_start(out_rows[:, b * share : (b + 1) * share, v0 : v0 + n], res[:])

        for u in range(2):
            join_low(0, u)
        fetch_left(1, 0)
        for t in range(PACK):
            if t + 1 < PACK:
                fetch_left(1, t + 1)
            shrink_terms(0, t, slice(0, HALF))
            fetch_right(1, t)
            if t == 0:
                z_bf0 = weave(0)
            if t == 2:
                join_low(1, 0)
        accs0 = open_sums(0)
        product(accs0, w2_q, quantize(z_bf0, HALF, "z0", "y2"), True)
        z2_bf0 = join_high(0)
        for t in range(PACK - 1):
            shrink_terms(1, t, slice(0, HALF))
        for part in (slice(0, P), slice(P, HALF)):
            shrink_terms(1, PACK - 1, part)
        join_low(1, 1)
        z_bf1 = weave(1)
        product(accs0, w3_q, quantize(z2_bf0, HALF, "z20"), False)
        store(0, accs0)
        z2_bf1 = join_high(1)
        z_q1 = quantize(z_bf1, HALF, "z1")
        accs1, accs2 = open_sums(1), open_sums(2)
        product(accs1, w2_q, z_q1, True, slice(0, P))
        product(accs2, w2_q, z_q1, True, slice(P, HALF))
        z2_bf2 = join_high(2)
        product(accs1, w3_q, quantize(z2_bf1, P, "z21"), False)
        store(1, accs1)
        product(accs2, w3_q, quantize(z2_bf2, P, "z22"), False)
        store(2, accs2)
